import numpy as np
import ml_dtypes


def mxq(x, axis, fmt="e4m3"):
    dtype, down = {"e4m3": (ml_dtypes.float8_e4m3fn, 7), "e5m2": (ml_dtypes.float8_e5m2, 14)}[fmt]
    v = np.moveaxis(np.asarray(x, np.float32).astype(ml_dtypes.bfloat16).astype(np.float64), axis, -1)
    blocks = v.reshape(v.shape[:-1] + (-1, 32))
    amax = np.abs(blocks).max(-1, keepdims=True)
    byte = np.maximum(np.where(amax > 0, np.frexp(amax)[1] - 1 + 127, 0) - down, 1)
    scale = np.exp2(byte - 127.0)
    codes = (blocks / scale).astype(np.float32).astype(dtype).astype(np.float64)
    return np.moveaxis((codes * scale).reshape(v.shape), -1, axis)


WIDE = False


def mx_kscale(k):
    if not WIDE:
        return np.ones(k)
    levels = np.array([10, -10, 5, -5, 0])
    if k % 512:
        return np.exp2(np.random.permutation(np.resize(levels, k // 32))).repeat(32)
    a = np.empty((k // 512, 16))
    for p in range(k // 512):
        a[p, :8] = np.random.permutation(np.resize(levels, 8))
        for g in range(8):
            far = levels[np.abs(levels - a[p, g]) >= 10]
            a[p, g + 8] = far[np.random.randint(len(far))]
    return np.exp2(a.ravel()).repeat(32)


def f64(x):
    return np.asarray(x).astype(np.float64)


def striped(idx):
    return np.tile(idx.reshape(-1, 16).T, (8, 1)).astype(np.uint16)


def unstriped(offs):
    return offs[:16].T.reshape(-1).astype(np.int64)


def relu(v):
    return np.maximum(v, 0.0)


K, T, S, D, V, N = 512, 1024, 512, 2, 256, 128
P = 2 ** 7


def setup_inputs():
    n = np.random.standard_normal
    s = mx_kscale(K)[:, None]
    return {
        "xT": (n((K, T)) * s).astype(np.float32),
        "w1": (n((K, N)) / np.sqrt(K) / s).astype(np.float32),
        "score": np.tile(np.random.standard_normal((D, 1, V)), (1, P, 1)).astype(np.float32),
        "offs": striped(np.random.permutation(T)[:S]),
        "pos1": striped(np.random.permutation(S)[:V]),
        "pos2": striped(np.random.permutation(S)[:V]),
    }


def reference(xT, w1, score, offs, pos1, pos2):
    xq = mxq(f64(xT)[:, unstriped(offs)], 0, "e4m3")
    y = mxq(f64(w1), 0, "e4m3").T @ xq
    e0 = np.exp(f64(score)[0, :1])
    e1 = np.exp(f64(score)[1, :1])
    num = y[:, unstriped(pos1)] * e0 + y[:, unstriped(pos2)] * e1
    den = e0 + e1
    return relu(num / den)

@@ -1,0 +1,140 @@
+from contextlib import ExitStack
+
+import concourse.mybir as mybir
+
+K, T, S, D, V, N = 512, 1024, 512, 2, 256, 128
+FLOPS = 2 * K * N * S
+
+F32 = mybir.dt.float32
+BF16 = mybir.dt.bfloat16
+U32 = mybir.dt.uint32
+U16 = mybir.dt.uint16
+U8 = mybir.dt.uint8
+FP8X4 = mybir.dt.float8_e4m3fn_x4
+ALU = mybir.AluOpType
+ACT = mybir.ActivationFunctionType
+
+P = 128
+PACK = 4
+LINE = 4
+CHUNKS = (
+    ((0, 512, 512), (512, 256, 256), (768, 256, 160)),
+    ((0, 256, 0), (256, 256, 0), (512, 256, 0), (768, 256, 256)),
+)
+PIECES = ((0, 256), (256, 128), (384, 128))
+
+
+def tile_picked_gatv_relu_e_kernel(tc, xT, w1, score, offs, pos1, pos2, out):
+    nc = tc.nc
+    with ExitStack() as ctx:
+        keep = ctx.enter_context(tc.tile_pool(name="keep", bufs=1))
+        psum = ctx.enter_context(tc.psum_pool(name="psum", bufs=1))
+
+        offs_sb = keep.tile([P, S // 16], U16, name="offs_sb")
+        pos1_sb = keep.tile([P, V // 16], U16, name="pos1_sb")
+        pos2_sb = keep.tile([P, V // 16], U16, name="pos2_sb")
+
+        warm_in = keep.tile([P, 1], F32, name="warm_in")
+        warm_out = keep.tile([P, 1], F32, name="warm_out")
+        nc.vector.memset(warm_in[:], 0.0)
+        nc.scalar.activation(warm_out[:], warm_in[:], ACT.Sigmoid)
+
+        x_rows = xT.rearrange("(p j) t -> p j t", j=PACK)
+        raw = {}
+        for u in range(2):
+            for c, (t0, width, on_vector) in enumerate(CHUNKS[u]):
+                raw[u, c] = keep.tile([P, 2, width], F32, name=f"raw{u}{c}")
+                nc.sync.dma_start(out=raw[u, c][:], in_=x_rows[:, 2 * u : 2 * u + 2, t0 : t0 + width])
+                if u == 0 and c == 0:
+                    nc.sync.dma_start(offs_sb[:], offs)
+        w_raw = keep.tile([P, PACK, N], F32, name="w_raw")
+        nc.sync.dma_start(out=w_raw[:], in_=w1.rearrange("(p j) m -> p j m", j=PACK))
+        score_sb = keep.tile([P, D, V], F32, name="score_sb")
+        nc.sync.dma_start(out=score_sb[:], in_=score.rearrange("d p v -> p d v"))
+        nc.sync.dma_start(pos1_sb[:], pos1)
+        nc.sync.dma_start(pos2_sb[:], pos2)
+
+        picked = [keep.tile([P, PACK * n], BF16, name=f"picked{i}", align_bytes=64) for i, (j0, n) in enumerate(PIECES)]
+        codes = [keep.tile([P, n], U32, name=f"codes{i}", align_bytes=64) for i, (j0, n) in enumerate(PIECES)]
+        scales = [keep.tile([P, n], U8, name=f"scales{i}", align_bytes=64) for i, (j0, n) in enumerate(PIECES)]
+        pairs = [keep.tile([P, 2 * T], BF16, name=f"pairs{u}", align_bytes=64) for u in range(2)]
+
+        def round_pairs(copy, u, c, lo, hi):
+            t0 = CHUNKS[u][c][0]
+            copy(
+                pairs[u][:, 2 * (t0 + lo) : 2 * (t0 + hi)].rearrange("p (c i e) -> p c e i", i=LINE, e=2),
+                raw[u, c][:, :, lo:hi].rearrange("p e (c i) -> p c e i", i=LINE),
+            )
+
+        def round_all(u):
+            for c, (t0, width, on_vector) in enumerate(CHUNKS[u]):
+                if on_vector > 0:
+                    round_pairs(nc.vector.tensor_copy, u, c, 0, on_vector)
+                if on_vector < width:
+                    round_pairs(nc.scalar.copy, u, c, on_vector, width)
+
+        def gather(u, i):
+            j0, n = PIECES[i]
+            nc.vector.tensor_copy(
+                picked[i][:].bitcast(U32).rearrange("p (n u) -> p n u", u=2)[:, :, u],
+                pairs[u][:].bitcast(U32).indirect(offs_sb[:, j0 // 16 : (j0 + n) // 16]),
+            )
+
+        def quantize(i):
+            nc.vector.quantize_mx(out=codes[i][:].bitcast(FP8X4), scales=scales[i][:], in_=picked[i][:])
+
+        round_all(0)
+        for i in range(len(PIECES)):
+            gather(0, i)
+        round_all(1)
+
+        w_grouped = keep.tile([P, PACK * N], BF16, name="w_grouped", align_bytes=64)
+        nc.scalar.copy(
+            w_grouped[:].rearrange("p (c i j) -> p c j i", i=LINE, j=PACK),
+            w_raw[:].rearrange("p j (c i) -> p c j i", i=LINE),
+        )
+        w_codes = keep.tile([P, N], U32, name="w_codes", align_bytes=64)
+        w_scales = keep.tile([P, N], U8, name="w_scales", align_bytes=64)
+
+        gather(1, 0)
+        gather(1, 1)
+        quantize(0)
+        nc.vector.quantize_mx(out=w_codes[:].bitcast(FP8X4), scales=w_scales[:], in_=w_grouped[:])
+        gather(1, 2)
+        quantize(1)
+        quantize(2)
+
+        gap = keep.tile([P, V], F32, name="gap")
+        nc.vector.tensor_tensor(gap[:], score_sb[:, 0, :], score_sb[:, 1, :], ALU.subtract)
+
+        y = keep.tile([P, S], F32, name="y")
+        for i, (j0, n) in enumerate(PIECES):
+            acc = psum.tile([P, n], F32, name=f"acc{i}")
+            nc.tensor.matmul_mx(
+                out=acc[:],
+                lhsT=w_codes[:].bitcast(FP8X4),
+                lhsT_scale=w_scales[:],
+                rhs=codes[i][:].bitcast(FP8X4),
+                rhs_scale=scales[i][:],
+                start=True,
+                stop=True,
+            )
+            if i < len(PIECES) - 1:
+                nc.scalar.copy(y[:, j0 : j0 + n], acc[:])
+            else:
+                nc.vector.tensor_copy(y[:, j0 : j0 + n], acc[:])
+
+        share0 = keep.tile([P, V], F32, name="share0")
+        share1 = keep.tile([P, V], F32, name="share1")
+        nc.scalar.activation(share0[:], gap[:], ACT.Sigmoid)
+        nc.scalar.activation(share1[:], gap[:], ACT.Sigmoid, scale=-1.0)
+
+        term0 = keep.tile([P, V], F32, name="term0")
+        term1 = keep.tile([P, V], F32, name="term1")
+        nc.vector.tensor_tensor(term0[:], y[:].indirect(pos1_sb[:]), share0[:], ALU.mult)
+        nc.vector.tensor_tensor(term1[:], y[:].indirect(pos2_sb[:]), share1[:], ALU.mult)
+        total = keep.tile([P, V], F32, name="total")
+        nc.vector.tensor_tensor(total[:], term0[:], term1[:], ALU.add)
+        result = keep.tile([P, V], F32, name="result")
+        nc.vector.tensor_scalar_max(result[:], total[:], 0.0)
+        nc.sync.dma_start(out=out, in_=result[:])

@@ -1,12 +1,14 @@
 from contextlib import ExitStack
 
 import concourse.mybir as mybir
+from concourse.masks import make_identity
 
 K, T, S, D, V, N = 512, 1024, 512, 2, 256, 128
 FLOPS = 2 * K * N * S
 
 F32 = mybir.dt.float32
 BF16 = mybir.dt.bfloat16
+I32 = mybir.dt.int32
 U32 = mybir.dt.uint32
 U16 = mybir.dt.uint16
 U8 = mybir.dt.uint8
@@ -17,11 +19,9 @@ ACT = mybir.ActivationFunctionType
 P = 128
 PACK = 4
 LINE = 4
-CHUNKS = (
-    ((0, 512, 512), (512, 256, 256), (768, 256, 160)),
-    ((0, 256, 0), (256, 256, 0), (512, 256, 0), (768, 256, 256)),
-)
-PIECES = ((0, 256), (256, 128), (384, 128))
+HALVES = V // P
+H = T // 2
+Q = T // 4
 
 
 def tile_picked_gatv_relu_e_kernel(tc, xT, w1, score, offs, pos1, pos2, out):
@@ -34,61 +34,82 @@ def tile_picked_gatv_relu_e_kernel(tc, xT, w1, score, offs, pos1, pos2, out):
         pos1_sb = keep.tile([P, V // 16], U16, name="pos1_sb")
         pos2_sb = keep.tile([P, V // 16], U16, name="pos2_sb")
 
-        warm_in = keep.tile([P, 1], F32, name="warm_in")
-        warm_out = keep.tile([P, 1], F32, name="warm_out")
-        nc.vector.memset(warm_in[:], 0.0)
-        nc.scalar.activation(warm_out[:], warm_in[:], ACT.Sigmoid)
+        score_rows = keep.tile([HALVES, D, P], F32, name="score_rows")
+        nc.scalar.dma_start(out=score_rows[:], in_=score[:, 0, :].rearrange("d (h c) -> h d c", c=P))
 
         x_rows = xT.rearrange("(p j) t -> p j t", j=PACK)
-        raw = {}
-        for u in range(2):
-            for c, (t0, width, on_vector) in enumerate(CHUNKS[u]):
-                raw[u, c] = keep.tile([P, 2, width], F32, name=f"raw{u}{c}")
-                nc.sync.dma_start(out=raw[u, c][:], in_=x_rows[:, 2 * u : 2 * u + 2, t0 : t0 + width])
-                if u == 0 and c == 0:
-                    nc.sync.dma_start(offs_sb[:], offs)
+        low = [keep.tile([P, T], F32, name=f"low{j}") for j in range(2)]
+        high_a = keep.tile([P, 2, H], F32, name="high_a")
+        high_b = keep.tile([P, 2, H], F32, name="high_b")
+        nc.sync.dma_start(offs_sb[:], offs)
+        for j in range(2):
+            nc.sync.dma_start(out=low[j][:], in_=x_rows[:, j, :])
+        nc.sync.dma_start(out=high_a[:], in_=x_rows[:, 2:4, 0:H])
+        nc.sync.dma_start(out=high_b[:, 0, :], in_=x_rows[:, 2, H:T])
+        nc.sync.dma_start(out=high_b[:, 1, 0:Q], in_=x_rows[:, 3, H : H + Q])
+        nc.sync.dma_start(out=high_b[:, 1, Q:H], in_=x_rows[:, 3, H + Q : T])
         w_raw = keep.tile([P, PACK, N], F32, name="w_raw")
         nc.sync.dma_start(out=w_raw[:], in_=w1.rearrange("(p j) m -> p j m", j=PACK))
-        score_sb = keep.tile([P, D, V], F32, name="score_sb")
-        nc.sync.dma_start(out=score_sb[:], in_=score.rearrange("d p v -> p d v"))
         nc.sync.dma_start(pos1_sb[:], pos1)
         nc.sync.dma_start(pos2_sb[:], pos2)
 
-        picked = [keep.tile([P, PACK * n], BF16, name=f"picked{i}", align_bytes=64) for i, (j0, n) in enumerate(PIECES)]
-        codes = [keep.tile([P, n], U32, name=f"codes{i}", align_bytes=64) for i, (j0, n) in enumerate(PIECES)]
-        scales = [keep.tile([P, n], U8, name=f"scales{i}", align_bytes=64) for i, (j0, n) in enumerate(PIECES)]
+        ident = keep.tile([P, P], F32, name="ident")
+        make_identity(nc, ident[:])
+        share_rows = keep.tile([P, D, P], F32, name="share_rows")
+        nc.gpsimd.memset(share_rows[:], 0.0)
+        gap_rows = keep.tile([HALVES, P], F32, name="gap_rows")
+        nc.vector.tensor_tensor(gap_rows[:], score_rows[:, 0, :], score_rows[:, 1, :], ALU.subtract)
+        for d in range(D):
+            nc.scalar.activation(share_rows[0:HALVES, d, :], gap_rows[:], ACT.Sigmoid, scale=1.0 - 2.0 * d)
+        turned = psum.tile([P, D, P], F32, name="turned")
+        for d in range(D):
+            nc.tensor.transpose(turned[:, d, :], share_rows[:, d, :], ident[:])
+        share_cols = keep.tile([P, D, HALVES], F32, name="share_cols")
+        nc.scalar.copy(share_cols[:], turned[:, :, 0:HALVES])
+        spread = psum.tile([P, D, V], F32, name="spread")
+        for d in range(D):
+            for h in range(HALVES):
+                nc.tensor.transpose(
+                    spread[:, d, h * P : (h + 1) * P], share_cols[:, d, h : h + 1].to_broadcast([P, P]), ident[:]
+                )
+
         pairs = [keep.tile([P, 2 * T], BF16, name=f"pairs{u}", align_bytes=64) for u in range(2)]
 
-        def round_pairs(copy, u, c, lo, hi):
-            t0 = CHUNKS[u][c][0]
+        def round_pairs(copy, u, raw, first, lo, hi):
             copy(
-                pairs[u][:, 2 * (t0 + lo) : 2 * (t0 + hi)].rearrange("p (c i e) -> p c e i", i=LINE, e=2),
-                raw[u, c][:, :, lo:hi].rearrange("p e (c i) -> p c e i", i=LINE),
+                pairs[u][:, 2 * (first + lo) : 2 * (first + hi)].rearrange("p (c i e) -> p c e i", i=LINE, e=2),
+                raw[:, :, lo:hi].rearrange("p e (c i) -> p c e i", i=LINE),
             )
 
-        def round_all(u):
-            for c, (t0, width, on_vector) in enumerate(CHUNKS[u]):
-                if on_vector > 0:
-                    round_pairs(nc.vector.tensor_copy, u, c, 0, on_vector)
-                if on_vector < width:
-                    round_pairs(nc.scalar.copy, u, c, on_vector, width)
+        cut = 384
+        got = [
+            keep.tile([P, 2 * cut], I32, name="got_first", tag="share0"),
+            keep.tile([P, 2 * (S - cut)], I32, name="got_last"),
+        ]
 
-        def gather(u, i):
-            j0, n = PIECES[i]
+        def words(j0, j1):
+            both = got[j0 // cut][:].rearrange("p (u n) -> p u n", u=2)
+            return both[:, :, j0 % cut : j0 % cut + j1 - j0]
+
+        def gather(u, j0, j1):
             nc.vector.tensor_copy(
-                picked[i][:].bitcast(U32).rearrange("p (n u) -> p n u", u=2)[:, :, u],
-                pairs[u][:].bitcast(U32).indirect(offs_sb[:, j0 // 16 : (j0 + n) // 16]),
+                words(j0, j1)[:, u, :].bitcast(U32), pairs[u][:].bitcast(U32).indirect(offs_sb[:, j0 // 16 : j1 // 16])
             )
 
-        def quantize(i):
-            nc.vector.quantize_mx(out=codes[i][:].bitcast(FP8X4), scales=scales[i][:], in_=picked[i][:])
+        low_got = keep.tile([P, 2 * S], BF16, name="low_got")
+        nc.vector.tensor_copy(low_got[:, 0:S], low[0][:].indirect(offs_sb[:]))
+        for j0, j1 in ((0, 192), (192, 384), (384, 512)):
+            nc.vector.tensor_copy(low_got[:, S + j0 : S + j1], low[1][:].indirect(offs_sb[:, j0 // 16 : j1 // 16]))
+            nc.scalar.copy(
+                words(j0, j1)[:, 0, :].bitcast(BF16).rearrange("p (c i e) -> p c e i", i=LINE, e=2),
+                low_got[:].rearrange("p (e n) -> p e n", e=2)[:, :, j0:j1].rearrange("p e (c i) -> p c e i", i=LINE),
+            )
+        round_pairs(nc.vector.tensor_copy, 1, high_a, 0, 0, H)
+        round_pairs(nc.vector.tensor_copy, 1, high_b, H, 0, Q)
+        round_pairs(nc.vector.tensor_copy, 1, high_b, H, Q, 432)
+        round_pairs(nc.scalar.copy, 1, high_b, H, 432, H)
 
-        round_all(0)
-        for i in range(len(PIECES)):
-            gather(0, i)
-        round_all(1)
-
-        w_grouped = keep.tile([P, PACK * N], BF16, name="w_grouped", align_bytes=64)
+        w_grouped = keep.tile([P, PACK * N], BF16, name="w_grouped", tag="w_grouped", align_bytes=64)
         nc.scalar.copy(
             w_grouped[:].rearrange("p (c i j) -> p c j i", i=LINE, j=PACK),
             w_raw[:].rearrange("p j (c i) -> p c j i", i=LINE),
@@ -96,20 +117,41 @@ def tile_picked_gatv_relu_e_kernel(tc, xT, w1, score, offs, pos1, pos2, out):
         w_codes = keep.tile([P, N], U32, name="w_codes", align_bytes=64)
         w_scales = keep.tile([P, N], U8, name="w_scales", align_bytes=64)
 
-        gather(1, 0)
-        gather(1, 1)
-        quantize(0)
-        nc.vector.quantize_mx(out=w_codes[:].bitcast(FP8X4), scales=w_scales[:], in_=w_grouped[:])
-        gather(1, 2)
-        quantize(1)
-        quantize(2)
+        products = ((0, 128), (128, 256), (256, 384), (384, 512))
+        woven_tags = ("woven0", "woven1", "woven2", "w_grouped")
+        codes_tags = ("codes0", "codes1", "codes256", "woven1")
+        woven, codes, scales = {}, {}, {}
 
-        gap = keep.tile([P, V], F32, name="gap")
-        nc.vector.tensor_tensor(gap[:], score_sb[:, 0, :], score_sb[:, 1, :], ALU.subtract)
+        def weave(copy, word, i):
+            j0, j1 = products[i]
+            woven[i] = keep.tile([P, PACK * (j1 - j0)], BF16, name=f"woven{i}", tag=woven_tags[i], align_bytes=64)
+            copy(
+                woven[i][:].bitcast(word).rearrange("p (c i u) -> p c u i", i=LINE, u=2),
+                words(j0, j1).bitcast(word).rearrange("p u (c i) -> p c u i", i=LINE),
+            )
+
+        def quantize(i):
+            j0, j1 = products[i]
+            codes[i] = keep.tile([P, j1 - j0], U32, name=f"codes{i}", tag=codes_tags[i], align_bytes=64)
+            scales[i] = keep.tile([P, j1 - j0], U8, name=f"scales{i}", align_bytes=64)
+            nc.vector.quantize_mx(out=codes[i][:].bitcast(FP8X4), scales=scales[i][:], in_=woven[i][:])
+
+        for i in range(3):
+            gather(1, products[i][0], products[i][1])
+            weave(nc.scalar.copy, U32, i)
+        gather(1, 384, 512)
+        nc.vector.quantize_mx(out=w_codes[:].bitcast(FP8X4), scales=w_scales[:], in_=w_grouped[:])
+        quantize(0)
+        weave(nc.vector.tensor_copy, I32, 3)
+        for i in range(1, 4):
+            quantize(i)
+
+        share0 = keep.tile([P, V], F32, name="share0", tag="share0")
+        nc.scalar.copy(share0[:], spread[:, 0, :])
 
         y = keep.tile([P, S], F32, name="y")
-        for i, (j0, n) in enumerate(PIECES):
-            acc = psum.tile([P, n], F32, name=f"acc{i}")
+        for i, (j0, j1) in enumerate(products):
+            acc = psum.tile([P, j1 - j0], F32, name=f"acc{i}")
             nc.tensor.matmul_mx(
                 out=acc[:],
                 lhsT=w_codes[:].bitcast(FP8X4),
@@ -119,22 +161,25 @@ def tile_picked_gatv_relu_e_kernel(tc, xT, w1, score, offs, pos1, pos2, out):
                 start=True,
                 stop=True,
             )
-            if i < len(PIECES) - 1:
-                nc.scalar.copy(y[:, j0 : j0 + n], acc[:])
+            if i < len(products) - 1:
+                nc.scalar.copy(y[:, j0:j1], acc[:])
             else:
-                nc.vector.tensor_copy(y[:, j0 : j0 + n], acc[:])
+                nc.vector.tensor_copy(y[:, j0:j1], acc[:])
 
-        share0 = keep.tile([P, V], F32, name="share0")
-        share1 = keep.tile([P, V], F32, name="share1")
-        nc.scalar.activation(share0[:], gap[:], ACT.Sigmoid)
-        nc.scalar.activation(share1[:], gap[:], ACT.Sigmoid, scale=-1.0)
-
+        share1 = keep.tile([P, V], F32, name="share1", tag="codes256", align_bytes=64)
+        nc.scalar.copy(share1[:], spread[:, 1, :])
         term0 = keep.tile([P, V], F32, name="term0")
         term1 = keep.tile([P, V], F32, name="term1")
         nc.vector.tensor_tensor(term0[:], y[:].indirect(pos1_sb[:]), share0[:], ALU.mult)
-        nc.vector.tensor_tensor(term1[:], y[:].indirect(pos2_sb[:]), share1[:], ALU.mult)
+        for lo, hi in ((0, 128), (128, 256)):
+            nc.vector.tensor_tensor(
+                term1[:, lo:hi], y[:].indirect(pos2_sb[:, lo // 16 : hi // 16]), share1[:, lo:hi], ALU.mult
+            )
         total = keep.tile([P, V], F32, name="total")
-        nc.vector.tensor_tensor(total[:], term0[:], term1[:], ALU.add)
         result = keep.tile([P, V], F32, name="result")
-        nc.vector.tensor_scalar_max(result[:], total[:], 0.0)
-        nc.sync.dma_start(out=out, in_=result[:])
+        for lo, hi in ((0, 128), (128, 256)):
+            nc.vector.tensor_tensor(total[:, lo:hi], term0[:, lo:hi], term1[:, lo:hi], ALU.add)
+        for lo, hi in ((0, 128), (128, 256)):
+            nc.vector.tensor_scalar_max(result[:, lo:hi], total[:, lo:hi], 0.0)
+        nc.sync.dma_start(out=out[:, 0:128], in_=result[:, 0:128])
+        nc.scalar.dma_start(out=out[:, 128:256], in_=result[:, 128:256])

@@ -22,12 +22,14 @@ LINE = 4
 HALVES = V // P
 H = T // 2
 Q = T // 4
+KIB = 1024
 
 
 def tile_picked_gatv_relu_e_kernel(tc, xT, w1, score, offs, pos1, pos2, out):
     nc = tc.nc
     with ExitStack() as ctx:
         keep = ctx.enter_context(tc.tile_pool(name="keep", bufs=1))
+        laid = ctx.enter_context(tc.tile_pool(name="laid", bufs=1))
         psum = ctx.enter_context(tc.psum_pool(name="psum", bufs=1))
 
         offs_sb = keep.tile([P, S // 16], U16, name="offs_sb")
@@ -39,119 +41,125 @@ def tile_picked_gatv_relu_e_kernel(tc, xT, w1, score, offs, pos1, pos2, out):
 
         x_rows = xT.rearrange("(p j) t -> p j t", j=PACK)
         low = [keep.tile([P, T], F32, name=f"low{j}") for j in range(2)]
-        high_a = keep.tile([P, 2, H], F32, name="high_a")
-        high_b = keep.tile([P, 2, H], F32, name="high_b")
+        high = keep.tile([P, 2 * T], F32, name="high")
+        high_planes = high[:].rearrange("p (e t) -> p e t", e=2)
         nc.sync.dma_start(offs_sb[:], offs)
         for j in range(2):
             nc.sync.dma_start(out=low[j][:], in_=x_rows[:, j, :])
-        nc.sync.dma_start(out=high_a[:], in_=x_rows[:, 2:4, 0:H])
-        nc.sync.dma_start(out=high_b[:, 0, :], in_=x_rows[:, 2, H:T])
-        nc.sync.dma_start(out=high_b[:, 1, 0:Q], in_=x_rows[:, 3, H : H + Q])
-        nc.sync.dma_start(out=high_b[:, 1, Q:H], in_=x_rows[:, 3, H + Q : T])
-        w_raw = keep.tile([P, PACK, N], F32, name="w_raw")
+        nc.sync.dma_start(out=high[:, 0:T], in_=x_rows[:, 2, :])
+        for t0, t1 in ((0, H), (H, H + Q), (H + Q, T)):
+            nc.sync.dma_start(out=high[:, T + t0 : T + t1], in_=x_rows[:, 3, t0:t1])
+        w_raw = laid.tile([P, PACK, N], F32, name="w_raw", offset=10 * KIB, align_bytes=64)
         nc.sync.dma_start(out=w_raw[:], in_=w1.rearrange("(p j) m -> p j m", j=PACK))
         nc.sync.dma_start(pos1_sb[:], pos1)
         nc.sync.dma_start(pos2_sb[:], pos2)
 
         ident = keep.tile([P, P], F32, name="ident")
         make_identity(nc, ident[:])
-        share_rows = keep.tile([P, D, P], F32, name="share_rows")
-        nc.gpsimd.memset(share_rows[:], 0.0)
+        half_tile = laid.tile([P, 10 * KIB // 4], F32, name="half_tile", offset=0, align_bytes=64)
+        half = half_tile[:, 0:1]
+        nc.vector.memset(half, 0.5)
+        lean_rows = keep.tile([P, P], F32, name="lean_rows")
+        nc.scalar.activation(lean_rows[:], half.to_broadcast([P, P]), ACT.Copy)
         gap_rows = keep.tile([HALVES, P], F32, name="gap_rows")
         nc.vector.tensor_tensor(gap_rows[:], score_rows[:, 0, :], score_rows[:, 1, :], ALU.subtract)
-        for d in range(D):
-            nc.scalar.activation(share_rows[0:HALVES, d, :], gap_rows[:], ACT.Sigmoid, scale=1.0 - 2.0 * d)
-        turned = psum.tile([P, D, P], F32, name="turned")
-        for d in range(D):
-            nc.tensor.transpose(turned[:, d, :], share_rows[:, d, :], ident[:])
-        share_cols = keep.tile([P, D, HALVES], F32, name="share_cols")
-        nc.scalar.copy(share_cols[:], turned[:, :, 0:HALVES])
-        spread = psum.tile([P, D, V], F32, name="spread")
-        for d in range(D):
-            for h in range(HALVES):
-                nc.tensor.transpose(
-                    spread[:, d, h * P : (h + 1) * P], share_cols[:, d, h : h + 1].to_broadcast([P, P]), ident[:]
-                )
+        nc.scalar.activation(lean_rows[0:HALVES, :], gap_rows[:], ACT.Tanh, scale=0.5)
+        turned = psum.tile([P, P], F32, name="turned")
+        nc.tensor.transpose(turned[:], lean_rows[:], ident[:])
+        lean_cols = keep.tile([P, HALVES], F32, name="lean_cols")
+        nc.scalar.copy(lean_cols[:], turned[:, 0:HALVES])
+        spread = psum.tile([P, V], F32, name="spread")
+        for h in range(HALVES):
+            nc.tensor.transpose(spread[:, h * P : (h + 1) * P], lean_cols[:, h : h + 1].to_broadcast([P, P]), ident[:])
+        share0 = keep.tile([P, V], F32, name="share0")
+        share1 = keep.tile([P, V], F32, name="share1")
+        nc.scalar.activation(share0[:], spread[:], ACT.Identity, scale=0.5, bias=half)
+        nc.scalar.activation(share1[:], spread[:], ACT.Identity, scale=-0.5, bias=half)
 
-        pairs = [keep.tile([P, 2 * T], BF16, name=f"pairs{u}", align_bytes=64) for u in range(2)]
+        def entries(i0, i1):
+            return offs_sb[:, i0 * P // 16 : i1 * P // 16]
 
-        def round_pairs(copy, u, raw, first, lo, hi):
-            copy(
-                pairs[u][:, 2 * (first + lo) : 2 * (first + hi)].rearrange("p (c i e) -> p c e i", i=LINE, e=2),
-                raw[:, :, lo:hi].rearrange("p e (c i) -> p c e i", i=LINE),
-            )
+        stage = [laid.tile([P, PACK * P], BF16, name=f"stage{i}", offset=i * KIB, align_bytes=64) for i in range(4)]
 
-        cut = 384
-        got = [
-            keep.tile([P, 2 * cut], I32, name="got_first", tag="share0"),
-            keep.tile([P, 2 * (S - cut)], I32, name="got_last"),
-        ]
+        def staged(i):
+            return stage[i][:]
 
-        def words(j0, j1):
-            both = got[j0 // cut][:].rearrange("p (u n) -> p u n", u=2)
-            return both[:, :, j0 % cut : j0 % cut + j1 - j0]
-
-        def gather(u, j0, j1):
-            nc.vector.tensor_copy(
-                words(j0, j1)[:, u, :].bitcast(U32), pairs[u][:].bitcast(U32).indirect(offs_sb[:, j0 // 16 : j1 // 16])
-            )
+        def slots(i):
+            return staged(i).rearrange("p (c i j) -> p c j i", i=LINE, j=PACK)
 
         low_got = keep.tile([P, 2 * S], BF16, name="low_got")
+        low_planes = low_got[:].rearrange("p (e n) -> p e n", e=2)
         nc.vector.tensor_copy(low_got[:, 0:S], low[0][:].indirect(offs_sb[:]))
-        for j0, j1 in ((0, 192), (192, 384), (384, 512)):
-            nc.vector.tensor_copy(low_got[:, S + j0 : S + j1], low[1][:].indirect(offs_sb[:, j0 // 16 : j1 // 16]))
-            nc.scalar.copy(
-                words(j0, j1)[:, 0, :].bitcast(BF16).rearrange("p (c i e) -> p c e i", i=LINE, e=2),
-                low_got[:].rearrange("p (e n) -> p e n", e=2)[:, :, j0:j1].rearrange("p e (c i) -> p c e i", i=LINE),
-            )
-        round_pairs(nc.vector.tensor_copy, 1, high_a, 0, 0, H)
-        round_pairs(nc.vector.tensor_copy, 1, high_b, H, 0, Q)
-        round_pairs(nc.vector.tensor_copy, 1, high_b, H, Q, 432)
-        round_pairs(nc.scalar.copy, 1, high_b, H, 432, H)
+        for i0, i1 in ((0, 1), (1, 3), (3, 4)):
+            nc.vector.tensor_copy(low_got[:, S + i0 * P : S + i1 * P], low[1][:].indirect(entries(i0, i1)))
+            for i in range(i0, i1):
+                if i > 0:
+                    dst = staged(i)[:, 0 : 2 * P].rearrange("p (c i e) -> p c e i", i=LINE, e=2)
+                else:
+                    dst = slots(i)[:, :, 0:2, :]
+                nc.scalar.copy(dst, low_planes[:, :, i * P : (i + 1) * P].rearrange("p e (c i) -> p c e i", i=LINE))
 
-        w_grouped = keep.tile([P, PACK * N], BF16, name="w_grouped", tag="w_grouped", align_bytes=64)
+        pairs = laid.tile([P, 2 * T], BF16, name="pairs", offset=4 * KIB, align_bytes=64)
+
+        def round_pairs(copy, t0, t1):
+            copy(
+                pairs[:, 2 * t0 : 2 * t1].rearrange("p (c i e) -> p c e i", i=LINE, e=2),
+                high_planes[:, :, t0:t1].rearrange("p e (c i) -> p c e i", i=LINE),
+            )
+
+        first, last = 512, 864
+        direct = laid.tile([P, 2 * P], F32, name="direct", offset=8 * KIB, align_bytes=64)
+        nc.vector.tensor_copy(direct[:, 0:P], high[:, 0:T].indirect(entries(0, 1)))
+        round_pairs(nc.vector.tensor_copy, 0, first)
+        round_pairs(nc.vector.tensor_copy, H, H + Q)
+        round_pairs(nc.vector.tensor_copy, H + Q, last)
+        round_pairs(nc.scalar.copy, last, T)
+        nc.vector.tensor_copy(direct[:, P : 2 * P], high[:, T : 2 * T].indirect(entries(0, 1)))
+
+        w_grouped = laid.tile([P, PACK * N], BF16, name="w_grouped", offset=9 * KIB, align_bytes=64)
         nc.scalar.copy(
             w_grouped[:].rearrange("p (c i j) -> p c j i", i=LINE, j=PACK),
             w_raw[:].rearrange("p j (c i) -> p c j i", i=LINE),
         )
+        nc.scalar.copy(
+            slots(0)[:, :, 2:4, :],
+            direct[:].rearrange("p (e c i) -> p c e i", e=2, i=LINE),
+        )
         w_codes = keep.tile([P, N], U32, name="w_codes", align_bytes=64)
         w_scales = keep.tile([P, N], U8, name="w_scales", align_bytes=64)
 
-        products = ((0, 128), (128, 256), (256, 384), (384, 512))
-        woven_tags = ("woven0", "woven1", "woven2", "w_grouped")
-        codes_tags = ("codes0", "codes1", "codes256", "woven1")
-        woven, codes, scales = {}, {}, {}
-
-        def weave(copy, word, i):
-            j0, j1 = products[i]
-            woven[i] = keep.tile([P, PACK * (j1 - j0)], BF16, name=f"woven{i}", tag=woven_tags[i], align_bytes=64)
-            copy(
-                woven[i][:].bitcast(word).rearrange("p (c i u) -> p c u i", i=LINE, u=2),
-                words(j0, j1).bitcast(word).rearrange("p u (c i) -> p c u i", i=LINE),
+        words = pairs[:].bitcast(U32)
+        late = [laid.tile([P, PACK * P], BF16, name=f"late{i}", offset=(10 + i) * KIB, align_bytes=64) for i in range(2)]
+        woven3 = keep.tile([P, PACK * P], BF16, name="woven3", align_bytes=64)
+        woven = {0: staged(0), 1: late[0][:], 2: late[1][:], 3: woven3[:]}
+        nc.vector.tensor_copy(staged(3).bitcast(U32)[:, P : 2 * P], words.indirect(entries(3, 4)))
+        for i in (1, 2):
+            nc.vector.tensor_copy(staged(i).bitcast(U32)[:, P : 2 * P], words.indirect(entries(i, i + 1)))
+            nc.scalar.copy(
+                woven[i].bitcast(U32).rearrange("p (c i u) -> p c u i", i=LINE, u=2),
+                staged(i).bitcast(U32).rearrange("p (u c i) -> p c u i", i=LINE, u=2),
             )
 
+        nc.vector.tensor_copy(
+            woven[3].bitcast(I32).rearrange("p (c i u) -> p c u i", i=LINE, u=2),
+            staged(3).bitcast(I32).rearrange("p (u c i) -> p c u i", i=LINE, u=2),
+        )
+        codes, scales = {}, {}
+
         def quantize(i):
-            j0, j1 = products[i]
-            codes[i] = keep.tile([P, j1 - j0], U32, name=f"codes{i}", tag=codes_tags[i], align_bytes=64)
-            scales[i] = keep.tile([P, j1 - j0], U8, name=f"scales{i}", align_bytes=64)
-            nc.vector.quantize_mx(out=codes[i][:].bitcast(FP8X4), scales=scales[i][:], in_=woven[i][:])
+            codes[i] = keep.tile([P, P], U32, name=f"codes{i}", align_bytes=64)
+            scales[i] = keep.tile([P, P], U8, name=f"scales{i}", align_bytes=64)
+            nc.vector.quantize_mx(out=codes[i][:].bitcast(FP8X4), scales=scales[i][:], in_=woven[i])
 
-        for i in range(3):
-            gather(1, products[i][0], products[i][1])
-            weave(nc.scalar.copy, U32, i)
-        gather(1, 384, 512)
         nc.vector.quantize_mx(out=w_codes[:].bitcast(FP8X4), scales=w_scales[:], in_=w_grouped[:])
+        quantize(3)
         quantize(0)
-        weave(nc.vector.tensor_copy, I32, 3)
-        for i in range(1, 4):
-            quantize(i)
-
-        share0 = keep.tile([P, V], F32, name="share0", tag="share0")
-        nc.scalar.copy(share0[:], spread[:, 0, :])
+        quantize(1)
+        quantize(2)
 
         y = keep.tile([P, S], F32, name="y")
-        for i, (j0, j1) in enumerate(products):
-            acc = psum.tile([P, j1 - j0], F32, name=f"acc{i}")
+        for i in (3, 0, 1, 2):
+            acc = psum.tile([P, P], F32, name=f"acc{i}")
             nc.tensor.matmul_mx(
                 out=acc[:],
                 lhsT=w_codes[:].bitcast(FP8X4),
@@ -161,13 +169,8 @@ def tile_picked_gatv_relu_e_kernel(tc, xT, w1, score, offs, pos1, pos2, out):
                 start=True,
                 stop=True,
             )
-            if i < len(products) - 1:
-                nc.scalar.copy(y[:, j0:j1], acc[:])
-            else:
-                nc.vector.tensor_copy(y[:, j0:j1], acc[:])
+            nc.scalar.copy(y[:, i * P : (i + 1) * P], acc[:])
 
-        share1 = keep.tile([P, V], F32, name="share1", tag="codes256", align_bytes=64)
-        nc.scalar.copy(share1[:], spread[:, 1, :])
         term0 = keep.tile([P, V], F32, name="term0")
         term1 = keep.tile([P, V], F32, name="term1")
         nc.vector.tensor_tensor(term0[:], y[:].indirect(pos1_sb[:]), share0[:], ALU.mult)
@@ -182,4 +185,4 @@ def tile_picked_gatv_relu_e_kernel(tc, xT, w1, score, offs, pos1, pos2, out):
         for lo, hi in ((0, 128), (128, 256)):
             nc.vector.tensor_scalar_max(result[:, lo:hi], total[:, lo:hi], 0.0)
         nc.sync.dma_start(out=out[:, 0:128], in_=result[:, 0:128])
-        nc.scalar.dma_start(out=out[:, 128:256], in_=result[:, 128:256])
+        nc.sync.dma_start(out=out[:, 128:256], in_=result[:, 128:256])

@@ -36,16 +36,22 @@ def tile_picked_gatv_relu_e_kernel(tc, xT, w1, score, offs, pos1, pos2, out):
         pos1_sb = keep.tile([P, V // 16], U16, name="pos1_sb")
         pos2_sb = keep.tile([P, V // 16], U16, name="pos2_sb")
 
-        score_rows = keep.tile([HALVES, D, P], F32, name="score_rows")
-        nc.scalar.dma_start(out=score_rows[:], in_=score[:, 0, :].rearrange("d (h c) -> h d c", c=P))
+
+        score_tile = laid.tile([P, 10 * KIB // 4], F32, name="score_tile", offset=0, align_bytes=64)
+        score_rows = score_tile[:, 0:P]
+        zero = keep.tile([P, 1], F32, name="zero")
+        nc.vector.memset(zero[:], 0.0)
+        nc.vector.memset(score_rows[0 : P // 2, :], 0.0)
+        nc.scalar.activation(score_rows[P // 2 :, :], zero[P // 2 :, :].to_broadcast([P // 2, P]), ACT.Copy)
 
         x_rows = xT.rearrange("(p j) t -> p j t", j=PACK)
         low = [keep.tile([P, T], F32, name=f"low{j}") for j in range(2)]
         high = keep.tile([P, 2 * T], F32, name="high")
         high_planes = high[:].rearrange("p (e t) -> p e t", e=2)
+        nc.sync.dma_start(out=low[0][:], in_=x_rows[:, 0, :])
         nc.sync.dma_start(offs_sb[:], offs)
-        for j in range(2):
-            nc.sync.dma_start(out=low[j][:], in_=x_rows[:, j, :])
+        nc.sync.dma_start(out=score_rows[0 : D * HALVES, :], in_=score[:, 0, :].rearrange("d (h c) -> d h c", c=P))
+        nc.sync.dma_start(out=low[1][:], in_=x_rows[:, 1, :])
         nc.sync.dma_start(out=high[:, 0:T], in_=x_rows[:, 2, :])
         for t0, t1 in ((0, H), (H, H + Q), (H + Q, T)):
             nc.sync.dma_start(out=high[:, T + t0 : T + t1], in_=x_rows[:, 3, t0:t1])
@@ -56,48 +62,36 @@ def tile_picked_gatv_relu_e_kernel(tc, xT, w1, score, offs, pos1, pos2, out):
 
         ident = keep.tile([P, P], F32, name="ident")
         make_identity(nc, ident[:])
-        half_tile = laid.tile([P, 10 * KIB // 4], F32, name="half_tile", offset=0, align_bytes=64)
-        half = half_tile[:, 0:1]
-        nc.vector.memset(half, 0.5)
-        lean_rows = keep.tile([P, P], F32, name="lean_rows")
-        nc.scalar.activation(lean_rows[:], half.to_broadcast([P, P]), ACT.Copy)
-        gap_rows = keep.tile([HALVES, P], F32, name="gap_rows")
-        nc.vector.tensor_tensor(gap_rows[:], score_rows[:, 0, :], score_rows[:, 1, :], ALU.subtract)
-        nc.scalar.activation(lean_rows[0:HALVES, :], gap_rows[:], ACT.Tanh, scale=0.5)
         turned = psum.tile([P, P], F32, name="turned")
-        nc.tensor.transpose(turned[:], lean_rows[:], ident[:])
+        nc.tensor.transpose(turned[:], score_rows, ident[:])
+        minus = keep.tile([P, HALVES], F32, name="minus")
+        nc.scalar.activation(minus[:], turned[:, HALVES : 2 * HALVES], ACT.Copy, scale=-0.5)
         lean_cols = keep.tile([P, HALVES], F32, name="lean_cols")
-        nc.scalar.copy(lean_cols[:], turned[:, 0:HALVES])
+        for h in range(HALVES):
+            nc.scalar.activation(lean_cols[:, h : h + 1], turned[:, h : h + 1], ACT.Tanh, scale=0.5, bias=minus[:, h : h + 1])
         spread = psum.tile([P, V], F32, name="spread")
         for h in range(HALVES):
             nc.tensor.transpose(spread[:, h * P : (h + 1) * P], lean_cols[:, h : h + 1].to_broadcast([P, P]), ident[:])
-        share0 = keep.tile([P, V], F32, name="share0")
-        share1 = keep.tile([P, V], F32, name="share1")
-        nc.scalar.activation(share0[:], spread[:], ACT.Identity, scale=0.5, bias=half)
-        nc.scalar.activation(share1[:], spread[:], ACT.Identity, scale=-0.5, bias=half)
 
-        def entries(i0, i1):
-            return offs_sb[:, i0 * P // 16 : i1 * P // 16]
+        def entries(n0, n1):
+            return offs_sb[:, n0 // 16 : n1 // 16]
 
-        stage = [laid.tile([P, PACK * P], BF16, name=f"stage{i}", offset=i * KIB, align_bytes=64) for i in range(4)]
-
-        def staged(i):
-            return stage[i][:]
-
-        def slots(i):
-            return staged(i).rearrange("p (c i j) -> p c j i", i=LINE, j=PACK)
+        cut = 320
+        woven_first = laid.tile([P, PACK * P], BF16, name="woven_first", offset=0, align_bytes=64)
+        words_mid = laid.tile([P, 2 * (cut - P)], I32, name="words_mid", offset=8 * P, align_bytes=64)
+        words_last = laid.tile([P, 2 * (S - cut)], I32, name="words_last", offset=8 * cut, align_bytes=64)
+        slots_first = woven_first[:].rearrange("p (c i j) -> p c j i", i=LINE, j=PACK)
 
         low_got = keep.tile([P, 2 * S], BF16, name="low_got")
         low_planes = low_got[:].rearrange("p (e n) -> p e n", e=2)
         nc.vector.tensor_copy(low_got[:, 0:S], low[0][:].indirect(offs_sb[:]))
-        for i0, i1 in ((0, 1), (1, 3), (3, 4)):
-            nc.vector.tensor_copy(low_got[:, S + i0 * P : S + i1 * P], low[1][:].indirect(entries(i0, i1)))
-            for i in range(i0, i1):
-                if i > 0:
-                    dst = staged(i)[:, 0 : 2 * P].rearrange("p (c i e) -> p c e i", i=LINE, e=2)
-                else:
-                    dst = slots(i)[:, :, 0:2, :]
-                nc.scalar.copy(dst, low_planes[:, :, i * P : (i + 1) * P].rearrange("p e (c i) -> p c e i", i=LINE))
+        for n0, n1, words in ((0, P, None), (P, cut, words_mid), (cut, S, words_last)):
+            nc.vector.tensor_copy(low_got[:, S + n0 : S + n1], low[1][:].indirect(entries(n0, n1)))
+            if words is None:
+                dst = slots_first[:, :, 0:2, :]
+            else:
+                dst = words[:, 0 : n1 - n0].bitcast(BF16).rearrange("p (c i e) -> p c e i", i=LINE, e=2)
+            nc.scalar.copy(dst, low_planes[:, :, n0:n1].rearrange("p e (c i) -> p c e i", i=LINE))
 
         pairs = laid.tile([P, 2 * T], BF16, name="pairs", offset=4 * KIB, align_bytes=64)
 
@@ -107,70 +101,76 @@ def tile_picked_gatv_relu_e_kernel(tc, xT, w1, score, offs, pos1, pos2, out):
                 high_planes[:, :, t0:t1].rearrange("p e (c i) -> p c e i", i=LINE),
             )
 
-        first, last = 512, 864
+        first, last = 448, 864
         direct = laid.tile([P, 2 * P], F32, name="direct", offset=8 * KIB, align_bytes=64)
-        nc.vector.tensor_copy(direct[:, 0:P], high[:, 0:T].indirect(entries(0, 1)))
+        nc.vector.tensor_copy(direct[:, 0:P], high[:, 0:T].indirect(entries(0, P)))
         round_pairs(nc.vector.tensor_copy, 0, first)
         round_pairs(nc.vector.tensor_copy, H, H + Q)
         round_pairs(nc.vector.tensor_copy, H + Q, last)
+        round_pairs(nc.scalar.copy, first, H)
         round_pairs(nc.scalar.copy, last, T)
-        nc.vector.tensor_copy(direct[:, P : 2 * P], high[:, T : 2 * T].indirect(entries(0, 1)))
+        nc.vector.tensor_copy(direct[:, P : 2 * P], high[:, T : 2 * T].indirect(entries(0, P)))
 
         w_grouped = laid.tile([P, PACK * N], BF16, name="w_grouped", offset=9 * KIB, align_bytes=64)
         nc.scalar.copy(
             w_grouped[:].rearrange("p (c i j) -> p c j i", i=LINE, j=PACK),
             w_raw[:].rearrange("p j (c i) -> p c j i", i=LINE),
         )
-        nc.scalar.copy(
-            slots(0)[:, :, 2:4, :],
-            direct[:].rearrange("p (e c i) -> p c e i", e=2, i=LINE),
-        )
+        nc.scalar.copy(slots_first[:, :, 2:4, :], direct[:].rearrange("p (e c i) -> p c e i", e=2, i=LINE))
         w_codes = keep.tile([P, N], U32, name="w_codes", align_bytes=64)
         w_scales = keep.tile([P, N], U8, name="w_scales", align_bytes=64)
 
-        words = pairs[:].bitcast(U32)
-        late = [laid.tile([P, PACK * P], BF16, name=f"late{i}", offset=(10 + i) * KIB, align_bytes=64) for i in range(2)]
-        woven3 = keep.tile([P, PACK * P], BF16, name="woven3", align_bytes=64)
-        woven = {0: staged(0), 1: late[0][:], 2: late[1][:], 3: woven3[:]}
-        nc.vector.tensor_copy(staged(3).bitcast(U32)[:, P : 2 * P], words.indirect(entries(3, 4)))
-        for i in (1, 2):
-            nc.vector.tensor_copy(staged(i).bitcast(U32)[:, P : 2 * P], words.indirect(entries(i, i + 1)))
-            nc.scalar.copy(
-                woven[i].bitcast(U32).rearrange("p (c i u) -> p c u i", i=LINE, u=2),
-                staged(i).bitcast(U32).rearrange("p (u c i) -> p c u i", i=LINE, u=2),
+        window = pairs[:].bitcast(U32)
+        nc.vector.tensor_copy(words_last[:, S - cut :].bitcast(U32), window.indirect(entries(cut, S)))
+        nc.vector.tensor_copy(words_mid[:, cut - P :].bitcast(U32), window.indirect(entries(P, cut)))
+
+        def weave(copy, word, woven, words, n0, n1):
+            copy(
+                woven[:].bitcast(word).rearrange("p (c i u) -> p c u i", i=LINE, u=2),
+                words[:].bitcast(word).rearrange("p (u n) -> p u n", u=2)[:, :, n0:n1].rearrange(
+                    "p u (c i) -> p c u i", i=LINE
+                ),
             )
 
-        nc.vector.tensor_copy(
-            woven[3].bitcast(I32).rearrange("p (c i u) -> p c u i", i=LINE, u=2),
-            staged(3).bitcast(I32).rearrange("p (u c i) -> p c u i", i=LINE, u=2),
+        woven_b = laid.tile([P, PACK * P], BF16, name="woven_b", offset=10 * KIB, align_bytes=64)
+        woven_c = laid.tile([P, PACK * (cut - 2 * P)], BF16, name="woven_c", offset=11 * KIB, align_bytes=64)
+        woven_d = keep.tile([P, PACK * (S - cut)], BF16, name="woven_d", align_bytes=64)
+        weave(nc.scalar.copy, U32, woven_b, words_mid, 0, P)
+        weave(nc.scalar.copy, U32, woven_c, words_mid, P, cut - P)
+        weave(nc.vector.tensor_copy, I32, woven_d, words_last, 0, S - cut)
+
+        products = (
+            (cut, cut + P, woven_d[:, 0 : PACK * P]),
+            (0, P, woven_first[:]),
+            (cut + P, S, woven_d[:, PACK * P :]),
+            (P, 2 * P, woven_b[:]),
+            (2 * P, cut, woven_c[:]),
         )
-        codes, scales = {}, {}
-
-        def quantize(i):
-            codes[i] = keep.tile([P, P], U32, name=f"codes{i}", align_bytes=64)
-            scales[i] = keep.tile([P, P], U8, name=f"scales{i}", align_bytes=64)
-            nc.vector.quantize_mx(out=codes[i][:].bitcast(FP8X4), scales=scales[i][:], in_=woven[i])
-
         nc.vector.quantize_mx(out=w_codes[:].bitcast(FP8X4), scales=w_scales[:], in_=w_grouped[:])
-        quantize(3)
-        quantize(0)
-        quantize(1)
-        quantize(2)
+        codes, scales = [], []
+        for g, (n0, n1, woven) in enumerate(products):
+            codes.append(keep.tile([P, n1 - n0], U32, name=f"codes{g}", tag=f"codes{g}", align_bytes=64))
+            scales.append(keep.tile([P, n1 - n0], U8, name=f"scales{g}", align_bytes=64))
+            nc.vector.quantize_mx(out=codes[g][:].bitcast(FP8X4), scales=scales[g][:], in_=woven)
 
+        share0 = laid.tile([P, V], F32, name="share0", offset=8 * P, align_bytes=64)
+        nc.scalar.activation(share0[:], spread[:], ACT.Copy, scale=0.5, bias=0.5)
         y = keep.tile([P, S], F32, name="y")
-        for i in (3, 0, 1, 2):
-            acc = psum.tile([P, P], F32, name=f"acc{i}")
+        for g, (n0, n1, woven) in enumerate(products):
+            acc = psum.tile([P, n1 - n0], F32, name=f"acc{g}")
             nc.tensor.matmul_mx(
                 out=acc[:],
                 lhsT=w_codes[:].bitcast(FP8X4),
                 lhsT_scale=w_scales[:],
-                rhs=codes[i][:].bitcast(FP8X4),
-                rhs_scale=scales[i][:],
+                rhs=codes[g][:].bitcast(FP8X4),
+                rhs_scale=scales[g][:],
                 start=True,
                 stop=True,
             )
-            nc.scalar.copy(y[:, i * P : (i + 1) * P], acc[:])
+            nc.scalar.copy(y[:, n0:n1], acc[:])
 
+        share1 = keep.tile([P, V], F32, name="share1", tag="codes4", align_bytes=64)
+        nc.scalar.activation(share1[:], spread[:], ACT.Copy, scale=-0.5, bias=0.5)
         term0 = keep.tile([P, V], F32, name="term0")
         term1 = keep.tile([P, V], F32, name="term1")
         nc.vector.tensor_tensor(term0[:], y[:].indirect(pos1_sb[:]), share0[:], ALU.mult)

@@ -19,10 +19,25 @@ ACT = mybir.ActivationFunctionType
 P = 128
 PACK = 4
 LINE = 4
+GROUP = 16
 HALVES = V // P
 H = T // 2
 Q = T // 4
 KIB = 1024
+ENTRY_BYTES = 2 * PACK
+
+CUT = 320
+PAIR_FIRST = 448
+PAIR_LAST = 864
+
+AT_WOVEN_FIRST = 0
+AT_WORDS_MID = ENTRY_BYTES * P
+AT_WORDS_LAST = ENTRY_BYTES * CUT
+AT_PAIRS = 4 * KIB
+AT_DIRECT = 8 * KIB
+AT_W_GROUPED = 9 * KIB
+AT_W_RAW = 10 * KIB
+AT_WOVEN_C = 11 * KIB
 
 
 def tile_picked_gatv_relu_e_kernel(tc, xT, w1, score, offs, pos1, pos2, out):
@@ -32,12 +47,11 @@ def tile_picked_gatv_relu_e_kernel(tc, xT, w1, score, offs, pos1, pos2, out):
         laid = ctx.enter_context(tc.tile_pool(name="laid", bufs=1))
         psum = ctx.enter_context(tc.psum_pool(name="psum", bufs=1))
 
-        offs_sb = keep.tile([P, S // 16], U16, name="offs_sb")
-        pos1_sb = keep.tile([P, V // 16], U16, name="pos1_sb")
-        pos2_sb = keep.tile([P, V // 16], U16, name="pos2_sb")
+        offs_sb = keep.tile([P, S // GROUP], U16, name="offs_sb")
+        pos1_sb = keep.tile([P, V // GROUP], U16, name="pos1_sb")
+        pos2_sb = keep.tile([P, V // GROUP], U16, name="pos2_sb")
 
-
-        score_tile = laid.tile([P, 10 * KIB // 4], F32, name="score_tile", offset=0, align_bytes=64)
+        score_tile = laid.tile([P, AT_W_RAW // 4], F32, name="score_tile", offset=0, align_bytes=64)
         score_rows = score_tile[:, 0:P]
         zero = keep.tile([P, 1], F32, name="zero")
         nc.vector.memset(zero[:], 0.0)
@@ -55,7 +69,7 @@ def tile_picked_gatv_relu_e_kernel(tc, xT, w1, score, offs, pos1, pos2, out):
         nc.sync.dma_start(out=high[:, 0:T], in_=x_rows[:, 2, :])
         for t0, t1 in ((0, H), (H, H + Q), (H + Q, T)):
             nc.sync.dma_start(out=high[:, T + t0 : T + t1], in_=x_rows[:, 3, t0:t1])
-        w_raw = laid.tile([P, PACK, N], F32, name="w_raw", offset=10 * KIB, align_bytes=64)
+        w_raw = laid.tile([P, PACK, N], F32, name="w_raw", offset=AT_W_RAW, align_bytes=64)
         nc.sync.dma_start(out=w_raw[:], in_=w1.rearrange("(p j) m -> p j m", j=PACK))
         nc.sync.dma_start(pos1_sb[:], pos1)
         nc.sync.dma_start(pos2_sb[:], pos2)
@@ -68,50 +82,56 @@ def tile_picked_gatv_relu_e_kernel(tc, xT, w1, score, offs, pos1, pos2, out):
         nc.scalar.activation(minus[:], turned[:, HALVES : 2 * HALVES], ACT.Copy, scale=-0.5)
         lean_cols = keep.tile([P, HALVES], F32, name="lean_cols")
         for h in range(HALVES):
-            nc.scalar.activation(lean_cols[:, h : h + 1], turned[:, h : h + 1], ACT.Tanh, scale=0.5, bias=minus[:, h : h + 1])
+            nc.scalar.activation(
+                lean_cols[:, h : h + 1], turned[:, h : h + 1], ACT.Tanh, scale=0.5, bias=minus[:, h : h + 1]
+            )
         spread = psum.tile([P, V], F32, name="spread")
         for h in range(HALVES):
             nc.tensor.transpose(spread[:, h * P : (h + 1) * P], lean_cols[:, h : h + 1].to_broadcast([P, P]), ident[:])
 
         def entries(n0, n1):
-            return offs_sb[:, n0 // 16 : n1 // 16]
+            return offs_sb[:, n0 // GROUP : n1 // GROUP]
 
-        cut = 320
-        woven_first = laid.tile([P, PACK * P], BF16, name="woven_first", offset=0, align_bytes=64)
-        words_mid = laid.tile([P, 2 * (cut - P)], I32, name="words_mid", offset=8 * P, align_bytes=64)
-        words_last = laid.tile([P, 2 * (S - cut)], I32, name="words_last", offset=8 * cut, align_bytes=64)
+        def by_lines(planes):
+            return planes.rearrange("p e (c i) -> p c e i", i=LINE)
+
+        woven_first = laid.tile([P, PACK * P], BF16, name="woven_first", offset=AT_WOVEN_FIRST, align_bytes=64)
+        words_mid = laid.tile([P, 2 * (CUT - P)], I32, name="words_mid", offset=AT_WORDS_MID, align_bytes=64)
+        words_last = laid.tile([P, 2 * (S - CUT)], I32, name="words_last", offset=AT_WORDS_LAST, align_bytes=64)
         slots_first = woven_first[:].rearrange("p (c i j) -> p c j i", i=LINE, j=PACK)
+
+        def low_pairs(words, count):
+            return words[:, 0:count].bitcast(BF16).rearrange("p (c i e) -> p c e i", i=LINE, e=2)
 
         low_got = keep.tile([P, 2 * S], BF16, name="low_got")
         low_planes = low_got[:].rearrange("p (e n) -> p e n", e=2)
         nc.vector.tensor_copy(low_got[:, 0:S], low[0][:].indirect(offs_sb[:]))
-        for n0, n1, words in ((0, P, None), (P, cut, words_mid), (cut, S, words_last)):
+        for n0, n1, paired in (
+            (0, P, slots_first[:, :, 0:2, :]),
+            (P, CUT, low_pairs(words_mid, CUT - P)),
+            (CUT, S, low_pairs(words_last, S - CUT)),
+        ):
             nc.vector.tensor_copy(low_got[:, S + n0 : S + n1], low[1][:].indirect(entries(n0, n1)))
-            if words is None:
-                dst = slots_first[:, :, 0:2, :]
-            else:
-                dst = words[:, 0 : n1 - n0].bitcast(BF16).rearrange("p (c i e) -> p c e i", i=LINE, e=2)
-            nc.scalar.copy(dst, low_planes[:, :, n0:n1].rearrange("p e (c i) -> p c e i", i=LINE))
+            nc.scalar.copy(paired, by_lines(low_planes[:, :, n0:n1]))
 
-        pairs = laid.tile([P, 2 * T], BF16, name="pairs", offset=4 * KIB, align_bytes=64)
+        pairs = laid.tile([P, 2 * T], BF16, name="pairs", offset=AT_PAIRS, align_bytes=64)
 
         def round_pairs(copy, t0, t1):
             copy(
                 pairs[:, 2 * t0 : 2 * t1].rearrange("p (c i e) -> p c e i", i=LINE, e=2),
-                high_planes[:, :, t0:t1].rearrange("p e (c i) -> p c e i", i=LINE),
+                by_lines(high_planes[:, :, t0:t1]),
             )
 
-        first, last = 448, 864
-        direct = laid.tile([P, 2 * P], F32, name="direct", offset=8 * KIB, align_bytes=64)
+        direct = laid.tile([P, 2 * P], F32, name="direct", offset=AT_DIRECT, align_bytes=64)
         nc.vector.tensor_copy(direct[:, 0:P], high[:, 0:T].indirect(entries(0, P)))
-        round_pairs(nc.vector.tensor_copy, 0, first)
+        round_pairs(nc.vector.tensor_copy, 0, PAIR_FIRST)
         round_pairs(nc.vector.tensor_copy, H, H + Q)
-        round_pairs(nc.vector.tensor_copy, H + Q, last)
-        round_pairs(nc.scalar.copy, first, H)
-        round_pairs(nc.scalar.copy, last, T)
+        round_pairs(nc.vector.tensor_copy, H + Q, PAIR_LAST)
+        round_pairs(nc.scalar.copy, PAIR_FIRST, H)
+        round_pairs(nc.scalar.copy, PAIR_LAST, T)
         nc.vector.tensor_copy(direct[:, P : 2 * P], high[:, T : 2 * T].indirect(entries(0, P)))
 
-        w_grouped = laid.tile([P, PACK * N], BF16, name="w_grouped", offset=9 * KIB, align_bytes=64)
+        w_grouped = laid.tile([P, PACK * N], BF16, name="w_grouped", offset=AT_W_GROUPED, align_bytes=64)
         nc.scalar.copy(
             w_grouped[:].rearrange("p (c i j) -> p c j i", i=LINE, j=PACK),
             w_raw[:].rearrange("p j (c i) -> p c j i", i=LINE),
@@ -121,40 +141,39 @@ def tile_picked_gatv_relu_e_kernel(tc, xT, w1, score, offs, pos1, pos2, out):
         w_scales = keep.tile([P, N], U8, name="w_scales", align_bytes=64)
 
         window = pairs[:].bitcast(U32)
-        nc.vector.tensor_copy(words_last[:, S - cut :].bitcast(U32), window.indirect(entries(cut, S)))
-        nc.vector.tensor_copy(words_mid[:, cut - P :].bitcast(U32), window.indirect(entries(P, cut)))
+        nc.vector.tensor_copy(words_last[:, S - CUT :].bitcast(U32), window.indirect(entries(CUT, S)))
+        nc.vector.tensor_copy(words_mid[:, CUT - P :].bitcast(U32), window.indirect(entries(P, CUT)))
 
         def weave(copy, word, woven, words, n0, n1):
             copy(
                 woven[:].bitcast(word).rearrange("p (c i u) -> p c u i", i=LINE, u=2),
-                words[:].bitcast(word).rearrange("p (u n) -> p u n", u=2)[:, :, n0:n1].rearrange(
-                    "p u (c i) -> p c u i", i=LINE
-                ),
+                by_lines(words[:].bitcast(word).rearrange("p (u n) -> p u n", u=2)[:, :, n0:n1]),
             )
 
-        woven_b = laid.tile([P, PACK * P], BF16, name="woven_b", offset=10 * KIB, align_bytes=64)
-        woven_c = laid.tile([P, PACK * (cut - 2 * P)], BF16, name="woven_c", offset=11 * KIB, align_bytes=64)
-        woven_d = keep.tile([P, PACK * (S - cut)], BF16, name="woven_d", align_bytes=64)
+        woven_b = laid.tile([P, PACK * P], BF16, name="woven_b", offset=AT_W_RAW, align_bytes=64)
+        woven_c = laid.tile([P, PACK * (CUT - 2 * P)], BF16, name="woven_c", offset=AT_WOVEN_C, align_bytes=64)
+        woven_d = keep.tile([P, PACK * (S - CUT)], BF16, name="woven_d", align_bytes=64)
         weave(nc.scalar.copy, U32, woven_b, words_mid, 0, P)
-        weave(nc.scalar.copy, U32, woven_c, words_mid, P, cut - P)
-        weave(nc.vector.tensor_copy, I32, woven_d, words_last, 0, S - cut)
+        weave(nc.scalar.copy, U32, woven_c, words_mid, P, CUT - P)
+        nc.vector.quantize_mx(out=w_codes[:].bitcast(FP8X4), scales=w_scales[:], in_=w_grouped[:])
+        weave(nc.vector.tensor_copy, I32, woven_d, words_last, 0, S - CUT)
 
         products = (
-            (cut, cut + P, woven_d[:, 0 : PACK * P]),
             (0, P, woven_first[:]),
-            (cut + P, S, woven_d[:, PACK * P :]),
+            (CUT, CUT + P, woven_d[:, 0 : PACK * P]),
+            (CUT + P, S, woven_d[:, PACK * P :]),
             (P, 2 * P, woven_b[:]),
-            (2 * P, cut, woven_c[:]),
+            (2 * P, CUT, woven_c[:]),
         )
-        nc.vector.quantize_mx(out=w_codes[:].bitcast(FP8X4), scales=w_scales[:], in_=w_grouped[:])
         codes, scales = [], []
         for g, (n0, n1, woven) in enumerate(products):
             codes.append(keep.tile([P, n1 - n0], U32, name=f"codes{g}", tag=f"codes{g}", align_bytes=64))
             scales.append(keep.tile([P, n1 - n0], U8, name=f"scales{g}", align_bytes=64))
             nc.vector.quantize_mx(out=codes[g][:].bitcast(FP8X4), scales=scales[g][:], in_=woven)
 
-        share0 = laid.tile([P, V], F32, name="share0", offset=8 * P, align_bytes=64)
-        nc.scalar.activation(share0[:], spread[:], ACT.Copy, scale=0.5, bias=0.5)
+        share0 = laid.tile([P, V], F32, name="share0", offset=AT_WOVEN_C, align_bytes=64)
+        nc.vector.tensor_scalar(share0[:], spread[:], 0.5, 0.5, ALU.mult, ALU.add)
+
         y = keep.tile([P, S], F32, name="y")
         for g, (n0, n1, woven) in enumerate(products):
             acc = psum.tile([P, n1 - n0], F32, name=f"acc{g}")
@@ -169,20 +188,21 @@ def tile_picked_gatv_relu_e_kernel(tc, xT, w1, score, offs, pos1, pos2, out):
             )
             nc.scalar.copy(y[:, n0:n1], acc[:])
 
-        share1 = keep.tile([P, V], F32, name="share1", tag="codes4", align_bytes=64)
+        share1 = keep.tile([P, V], F32, name="share1", tag=f"codes{len(products) - 1}", align_bytes=64)
         nc.scalar.activation(share1[:], spread[:], ACT.Copy, scale=-0.5, bias=0.5)
+
+        halves = [slice(h * P, (h + 1) * P) for h in range(HALVES)]
         term0 = keep.tile([P, V], F32, name="term0")
         term1 = keep.tile([P, V], F32, name="term1")
         nc.vector.tensor_tensor(term0[:], y[:].indirect(pos1_sb[:]), share0[:], ALU.mult)
-        for lo, hi in ((0, 128), (128, 256)):
-            nc.vector.tensor_tensor(
-                term1[:, lo:hi], y[:].indirect(pos2_sb[:, lo // 16 : hi // 16]), share1[:, lo:hi], ALU.mult
-            )
+        for cols in halves:
+            picked = y[:].indirect(pos2_sb[:, cols.start // GROUP : cols.stop // GROUP])
+            nc.vector.tensor_tensor(term1[:, cols], picked, share1[:, cols], ALU.mult)
         total = keep.tile([P, V], F32, name="total")
         result = keep.tile([P, V], F32, name="result")
-        for lo, hi in ((0, 128), (128, 256)):
-            nc.vector.tensor_tensor(total[:, lo:hi], term0[:, lo:hi], term1[:, lo:hi], ALU.add)
-        for lo, hi in ((0, 128), (128, 256)):
-            nc.vector.tensor_scalar_max(result[:, lo:hi], total[:, lo:hi], 0.0)
-        nc.sync.dma_start(out=out[:, 0:128], in_=result[:, 0:128])
-        nc.sync.dma_start(out=out[:, 128:256], in_=result[:, 128:256])
+        for cols in halves:
+            nc.vector.tensor_tensor(total[:, cols], term0[:, cols], term1[:, cols], ALU.add)
+        for cols in halves:
+            nc.vector.tensor_scalar_max(result[:, cols], total[:, cols], 0.0)
+        for cols in halves:
+            nc.sync.dma_start(out=out[:, cols], in_=result[:, cols])

@@ -8,7 +8,6 @@ FLOPS = 2 * K * N * S
 
 F32 = mybir.dt.float32
 BF16 = mybir.dt.bfloat16
-I32 = mybir.dt.int32
 U32 = mybir.dt.uint32
 U16 = mybir.dt.uint16
 U8 = mybir.dt.uint8
@@ -21,23 +20,14 @@ PACK = 4
 LINE = 4
 GROUP = 16
 HALVES = V // P
-H = T // 2
-Q = T // 4
 KIB = 1024
-ENTRY_BYTES = 2 * PACK
 
-CUT = 320
-PAIR_FIRST = 448
-PAIR_LAST = 864
+AT_PLANE1 = 0
+AT_PLANE2 = 4 * KIB
+AT_GOT = 8 * KIB
 
-AT_WOVEN_FIRST = 0
-AT_WORDS_MID = ENTRY_BYTES * P
-AT_WORDS_LAST = ENTRY_BYTES * CUT
-AT_PAIRS = 4 * KIB
-AT_DIRECT = 8 * KIB
-AT_W_GROUPED = 9 * KIB
-AT_W_RAW = 10 * KIB
-AT_WOVEN_C = 11 * KIB
+CUT = 192
+PARTS = ((0, 2 * P), (2 * P, S))
 
 
 def tile_picked_gatv_relu_e_kernel(tc, xT, w1, score, offs, pos1, pos2, out):
@@ -51,33 +41,74 @@ def tile_picked_gatv_relu_e_kernel(tc, xT, w1, score, offs, pos1, pos2, out):
         pos1_sb = keep.tile([P, V // GROUP], U16, name="pos1_sb")
         pos2_sb = keep.tile([P, V // GROUP], U16, name="pos2_sb")
 
-        score_tile = laid.tile([P, AT_W_RAW // 4], F32, name="score_tile", offset=0, align_bytes=64)
-        score_rows = score_tile[:, 0:P]
+        score_rows = keep.tile([P, P], F32, name="score_rows")
         zero = keep.tile([P, 1], F32, name="zero")
         nc.vector.memset(zero[:], 0.0)
         nc.vector.memset(score_rows[0 : P // 2, :], 0.0)
         nc.scalar.activation(score_rows[P // 2 :, :], zero[P // 2 :, :].to_broadcast([P // 2, P]), ACT.Copy)
 
         x_rows = xT.rearrange("(p j) t -> p j t", j=PACK)
-        low = [keep.tile([P, T], F32, name=f"low{j}") for j in range(2)]
-        high = keep.tile([P, 2 * T], F32, name="high")
-        high_planes = high[:].rearrange("p (e t) -> p e t", e=2)
-        nc.sync.dma_start(out=low[0][:], in_=x_rows[:, 0, :])
+        planes = [
+            keep.tile([P, T], F32, name="plane0"),
+            laid.tile([P, T], F32, name="plane1", offset=AT_PLANE1, align_bytes=64),
+            laid.tile([P, T], F32, name="plane2", offset=AT_PLANE2, align_bytes=64),
+            keep.tile([P, T], F32, name="plane3"),
+        ]
+        nc.sync.dma_start(out=planes[0][:], in_=x_rows[:, 0, :])
         nc.sync.dma_start(offs_sb[:], offs)
         nc.sync.dma_start(out=score_rows[0 : D * HALVES, :], in_=score[:, 0, :].rearrange("d (h c) -> d h c", c=P))
-        nc.sync.dma_start(out=low[1][:], in_=x_rows[:, 1, :])
-        nc.sync.dma_start(out=high[:, 0:T], in_=x_rows[:, 2, :])
-        for t0, t1 in ((0, H), (H, H + Q), (H + Q, T)):
-            nc.sync.dma_start(out=high[:, T + t0 : T + t1], in_=x_rows[:, 3, t0:t1])
-        w_raw = laid.tile([P, PACK, N], F32, name="w_raw", offset=AT_W_RAW, align_bytes=64)
+        for j in range(1, PACK):
+            nc.sync.dma_start(out=planes[j][:], in_=x_rows[:, j, :])
+        w_raw = keep.tile([P, PACK, N], F32, name="w_raw")
         nc.sync.dma_start(out=w_raw[:], in_=w1.rearrange("(p j) m -> p j m", j=PACK))
-        nc.sync.dma_start(pos1_sb[:], pos1)
         nc.sync.dma_start(pos2_sb[:], pos2)
+        nc.sync.dma_start(pos1_sb[:], pos1)
 
         ident = keep.tile([P, P], F32, name="ident")
         make_identity(nc, ident[:])
         turned = psum.tile([P, P], F32, name="turned")
-        nc.tensor.transpose(turned[:], score_rows, ident[:])
+        nc.tensor.transpose(turned[:], score_rows[:], ident[:])
+
+        def entries(n0, n1):
+            return offs_sb[:, n0 // GROUP : n1 // GROUP]
+
+        woven = keep.tile([P, PACK * S], BF16, name="woven", align_bytes=64)
+
+        def got_tiles(u):
+            return [
+                laid.tile([P, 2 * (n1 - n0)], BF16, name=f"got{u}_{n0}", offset=AT_GOT + 4 * n0, align_bytes=64)
+                for n0, n1 in PARTS
+            ]
+
+        def slot(got, part, n0, n1):
+            first = PARTS[part][0]
+            return got[part][:].rearrange("p (e n) -> p e n", e=2)[:, :, n0 - first : n1 - first]
+
+        def weave(copy, u, got, part, n0, n1):
+            copy(
+                woven[:, PACK * n0 : PACK * n1].rearrange("p (c i j) -> p c j i", i=LINE, j=PACK)[:, :, 2 * u : 2 * u + 2, :],
+                slot(got, part, n0, n1).rearrange("p e (c i) -> p c e i", i=LINE),
+            )
+
+        def gather_v(got, j, n0, n1):
+            nc.vector.tensor_copy(slot(got, 0, n0, n1)[:, j % 2, :], planes[j][:].indirect(entries(n0, n1)))
+
+        def gather_s(got, j, n0, n1):
+            nc.scalar.activation(slot(got, 1, n0, n1)[:, j % 2, :], planes[j][:].indirect(entries(n0, n1)), ACT.Copy)
+
+        def first_plane(got, j):
+            gather_v(got, j, 0, 2 * P)
+            gather_s(got, j, 2 * P, S)
+
+        def second_plane(got, j):
+            gather_v(got, j, 0, P)
+            gather_v(got, j, P, 2 * P)
+            gather_s(got, j, 2 * P, 3 * P)
+            gather_s(got, j, 3 * P, S)
+
+        got = got_tiles(0)
+        first_plane(got, 0)
+
         minus = keep.tile([P, HALVES], F32, name="minus")
         nc.scalar.activation(minus[:], turned[:, HALVES : 2 * HALVES], ACT.Copy, scale=-0.5)
         lean_cols = keep.tile([P, HALVES], F32, name="lean_cols")
@@ -89,94 +120,41 @@ def tile_picked_gatv_relu_e_kernel(tc, xT, w1, score, offs, pos1, pos2, out):
         for h in range(HALVES):
             nc.tensor.transpose(spread[:, h * P : (h + 1) * P], lean_cols[:, h : h + 1].to_broadcast([P, P]), ident[:])
 
-        def entries(n0, n1):
-            return offs_sb[:, n0 // GROUP : n1 // GROUP]
-
-        def by_lines(planes):
-            return planes.rearrange("p e (c i) -> p c e i", i=LINE)
-
-        woven_first = laid.tile([P, PACK * P], BF16, name="woven_first", offset=AT_WOVEN_FIRST, align_bytes=64)
-        words_mid = laid.tile([P, 2 * (CUT - P)], I32, name="words_mid", offset=AT_WORDS_MID, align_bytes=64)
-        words_last = laid.tile([P, 2 * (S - CUT)], I32, name="words_last", offset=AT_WORDS_LAST, align_bytes=64)
-        slots_first = woven_first[:].rearrange("p (c i j) -> p c j i", i=LINE, j=PACK)
-
-        def low_pairs(words, count):
-            return words[:, 0:count].bitcast(BF16).rearrange("p (c i e) -> p c e i", i=LINE, e=2)
-
-        low_got = keep.tile([P, 2 * S], BF16, name="low_got")
-        low_planes = low_got[:].rearrange("p (e n) -> p e n", e=2)
-        nc.vector.tensor_copy(low_got[:, 0:S], low[0][:].indirect(offs_sb[:]))
-        for n0, n1, paired in (
-            (0, P, slots_first[:, :, 0:2, :]),
-            (P, CUT, low_pairs(words_mid, CUT - P)),
-            (CUT, S, low_pairs(words_last, S - CUT)),
-        ):
-            nc.vector.tensor_copy(low_got[:, S + n0 : S + n1], low[1][:].indirect(entries(n0, n1)))
-            nc.scalar.copy(paired, by_lines(low_planes[:, :, n0:n1]))
-
-        pairs = laid.tile([P, 2 * T], BF16, name="pairs", offset=AT_PAIRS, align_bytes=64)
-
-        def round_pairs(copy, t0, t1):
-            copy(
-                pairs[:, 2 * t0 : 2 * t1].rearrange("p (c i e) -> p c e i", i=LINE, e=2),
-                by_lines(high_planes[:, :, t0:t1]),
-            )
-
-        direct = laid.tile([P, 2 * P], F32, name="direct", offset=AT_DIRECT, align_bytes=64)
-        nc.vector.tensor_copy(direct[:, 0:P], high[:, 0:T].indirect(entries(0, P)))
-        round_pairs(nc.vector.tensor_copy, 0, PAIR_FIRST)
-        round_pairs(nc.vector.tensor_copy, H, H + Q)
-        round_pairs(nc.vector.tensor_copy, H + Q, PAIR_LAST)
-        round_pairs(nc.scalar.copy, PAIR_FIRST, H)
-        round_pairs(nc.scalar.copy, PAIR_LAST, T)
-        nc.vector.tensor_copy(direct[:, P : 2 * P], high[:, T : 2 * T].indirect(entries(0, P)))
-
-        w_grouped = laid.tile([P, PACK * N], BF16, name="w_grouped", offset=AT_W_GROUPED, align_bytes=64)
-        nc.scalar.copy(
-            w_grouped[:].rearrange("p (c i j) -> p c j i", i=LINE, j=PACK),
-            w_raw[:].rearrange("p j (c i) -> p c j i", i=LINE),
-        )
-        nc.scalar.copy(slots_first[:, :, 2:4, :], direct[:].rearrange("p (e c i) -> p c e i", e=2, i=LINE))
-        w_codes = keep.tile([P, N], U32, name="w_codes", align_bytes=64)
-        w_scales = keep.tile([P, N], U8, name="w_scales", align_bytes=64)
-
-        window = pairs[:].bitcast(U32)
-        nc.vector.tensor_copy(words_last[:, S - CUT :].bitcast(U32), window.indirect(entries(CUT, S)))
-        nc.vector.tensor_copy(words_mid[:, CUT - P :].bitcast(U32), window.indirect(entries(P, CUT)))
-
-        def weave(copy, word, woven, words, n0, n1):
-            copy(
-                woven[:].bitcast(word).rearrange("p (c i u) -> p c u i", i=LINE, u=2),
-                by_lines(words[:].bitcast(word).rearrange("p (u n) -> p u n", u=2)[:, :, n0:n1]),
-            )
-
-        woven_b = laid.tile([P, PACK * P], BF16, name="woven_b", offset=AT_W_RAW, align_bytes=64)
-        woven_c = laid.tile([P, PACK * (CUT - 2 * P)], BF16, name="woven_c", offset=AT_WOVEN_C, align_bytes=64)
-        woven_d = keep.tile([P, PACK * (S - CUT)], BF16, name="woven_d", align_bytes=64)
-        weave(nc.scalar.copy, U32, woven_b, words_mid, 0, P)
-        weave(nc.scalar.copy, U32, woven_c, words_mid, P, CUT - P)
-        nc.vector.quantize_mx(out=w_codes[:].bitcast(FP8X4), scales=w_scales[:], in_=w_grouped[:])
-        weave(nc.vector.tensor_copy, I32, woven_d, words_last, 0, S - CUT)
-
-        products = (
-            (0, P, woven_first[:]),
-            (CUT, CUT + P, woven_d[:, 0 : PACK * P]),
-            (CUT + P, S, woven_d[:, PACK * P :]),
-            (P, 2 * P, woven_b[:]),
-            (2 * P, CUT, woven_c[:]),
-        )
-        codes, scales = [], []
-        for g, (n0, n1, woven) in enumerate(products):
-            codes.append(keep.tile([P, n1 - n0], U32, name=f"codes{g}", tag=f"codes{g}", align_bytes=64))
-            scales.append(keep.tile([P, n1 - n0], U8, name=f"scales{g}", align_bytes=64))
-            nc.vector.quantize_mx(out=codes[g][:].bitcast(FP8X4), scales=scales[g][:], in_=woven)
-
-        share0 = laid.tile([P, V], F32, name="share0", offset=AT_WOVEN_C, align_bytes=64)
+        second_plane(got, 1)
+        weave(nc.scalar.copy, 0, got, 1, 2 * P, 3 * P)
+        weave(nc.vector.tensor_copy, 0, got, 0, 0, 2 * P)
+        weave(nc.vector.tensor_copy, 0, got, 1, 3 * P, S)
+        share0 = laid.tile([P, V], F32, name="share0", offset=AT_PLANE1, align_bytes=64)
         nc.vector.tensor_scalar(share0[:], spread[:], 0.5, 0.5, ALU.mult, ALU.add)
 
+        got = got_tiles(1)
+        first_plane(got, 2)
+        second_plane(got, 3)
+        weave(nc.scalar.copy, 1, got, 1, 2 * P, 3 * P)
+        weave(nc.scalar.copy, 1, got, 1, 3 * P, S)
+        weave(nc.scalar.copy, 1, got, 0, CUT, 2 * P)
+        weave(nc.vector.tensor_copy, 1, got, 0, 0, P)
+        w_woven = laid.tile([P, PACK * N], BF16, name="w_woven", offset=AT_PLANE2, align_bytes=64)
+        nc.vector.tensor_copy(
+            w_woven[:].rearrange("p (c i j) -> p c j i", i=LINE, j=PACK),
+            w_raw[:].rearrange("p j (c i) -> p c j i", i=LINE),
+        )
+        weave(nc.vector.tensor_copy, 1, got, 0, P, CUT)
+
+        products = [(n0, woven[:, PACK * n0 : PACK * (n0 + P)]) for n0 in (0, 2 * P, 3 * P, P)]
+        w_codes = keep.tile([P, N], U32, name="w_codes", align_bytes=64)
+        w_scales = keep.tile([P, N], U8, name="w_scales", align_bytes=64)
+        codes, scales = [], []
+        for g, (n0, values) in enumerate(products):
+            codes.append(keep.tile([P, P], U32, name=f"codes{g}", align_bytes=64))
+            scales.append(keep.tile([P, P], U8, name=f"scales{g}", align_bytes=64))
+            nc.vector.quantize_mx(out=codes[g][:].bitcast(FP8X4), scales=scales[g][:], in_=values)
+            if g == 0:
+                nc.vector.quantize_mx(out=w_codes[:].bitcast(FP8X4), scales=w_scales[:], in_=w_woven[:])
+
         y = keep.tile([P, S], F32, name="y")
-        for g, (n0, n1, woven) in enumerate(products):
-            acc = psum.tile([P, n1 - n0], F32, name=f"acc{g}")
+        for g, (n0, values) in enumerate(products):
+            acc = psum.tile([P, P], F32, name=f"acc{g}")
             nc.tensor.matmul_mx(
                 out=acc[:],
                 lhsT=w_codes[:].bitcast(FP8X4),
@@ -186,22 +164,22 @@ def tile_picked_gatv_relu_e_kernel(tc, xT, w1, score, offs, pos1, pos2, out):
                 start=True,
                 stop=True,
             )
-            nc.scalar.copy(y[:, n0:n1], acc[:])
-
-        share1 = keep.tile([P, V], F32, name="share1", tag=f"codes{len(products) - 1}", align_bytes=64)
-        nc.scalar.activation(share1[:], spread[:], ACT.Copy, scale=-0.5, bias=0.5)
+            nc.scalar.copy(y[:, n0 : n0 + P], acc[:])
 
         halves = [slice(h * P, (h + 1) * P) for h in range(HALVES)]
         term0 = keep.tile([P, V], F32, name="term0")
+        second = keep.tile([P, V], F32, name="second")
         term1 = keep.tile([P, V], F32, name="term1")
+        total = keep.tile([P, V], F32, name="total")
+        result = keep.tile([P, V], F32, name="result")
         nc.vector.tensor_tensor(term0[:], y[:].indirect(pos1_sb[:]), share0[:], ALU.mult)
         for cols in halves:
             picked = y[:].indirect(pos2_sb[:, cols.start // GROUP : cols.stop // GROUP])
-            nc.vector.tensor_tensor(term1[:, cols], picked, share1[:, cols], ALU.mult)
-        total = keep.tile([P, V], F32, name="total")
-        result = keep.tile([P, V], F32, name="result")
+            nc.scalar.activation(second[:, cols], picked, ACT.Copy)
         for cols in halves:
-            nc.vector.tensor_tensor(total[:, cols], term0[:, cols], term1[:, cols], ALU.add)
+            nc.vector.scalar_tensor_tensor(term1[:, cols], spread[:, cols], 1.0, second[:, cols], ALU.subtract, ALU.mult)
+        for cols in halves:
+            nc.vector.scalar_tensor_tensor(total[:, cols], term1[:, cols], -0.5, term0[:, cols], ALU.mult, ALU.add)
         for cols in halves:
             nc.vector.tensor_scalar_max(result[:, cols], total[:, cols], 0.0)
         for cols in halves:

@@ -22,19 +22,14 @@ GROUP = 16
 HALVES = V // P
 KIB = 1024
 
-AT_PLANE1 = 0
-AT_PLANE2 = 4 * KIB
-AT_GOT = 8 * KIB
-
-CUT = 192
-PARTS = ((0, 2 * P), (2 * P, S))
+EARLY_CUT = 320
+EARLY_WEAVE = 384
 
 
 def tile_picked_gatv_relu_e_kernel(tc, xT, w1, score, offs, pos1, pos2, out):
     nc = tc.nc
     with ExitStack() as ctx:
         keep = ctx.enter_context(tc.tile_pool(name="keep", bufs=1))
-        laid = ctx.enter_context(tc.tile_pool(name="laid", bufs=1))
         psum = ctx.enter_context(tc.psum_pool(name="psum", bufs=1))
 
         offs_sb = keep.tile([P, S // GROUP], U16, name="offs_sb")
@@ -48,12 +43,7 @@ def tile_picked_gatv_relu_e_kernel(tc, xT, w1, score, offs, pos1, pos2, out):
         nc.scalar.activation(score_rows[P // 2 :, :], zero[P // 2 :, :].to_broadcast([P // 2, P]), ACT.Copy)
 
         x_rows = xT.rearrange("(p j) t -> p j t", j=PACK)
-        planes = [
-            keep.tile([P, T], F32, name="plane0"),
-            laid.tile([P, T], F32, name="plane1", offset=AT_PLANE1, align_bytes=64),
-            laid.tile([P, T], F32, name="plane2", offset=AT_PLANE2, align_bytes=64),
-            keep.tile([P, T], F32, name="plane3"),
-        ]
+        planes = [keep.tile([P, T], F32, name=f"plane{j}") for j in range(PACK)]
         nc.sync.dma_start(out=planes[0][:], in_=x_rows[:, 0, :])
         nc.sync.dma_start(offs_sb[:], offs)
         nc.sync.dma_start(out=score_rows[0 : D * HALVES, :], in_=score[:, 0, :].rearrange("d (h c) -> d h c", c=P))
@@ -74,40 +64,27 @@ def tile_picked_gatv_relu_e_kernel(tc, xT, w1, score, offs, pos1, pos2, out):
 
         woven = keep.tile([P, PACK * S], BF16, name="woven", align_bytes=64)
 
-        def got_tiles(u):
-            return [
-                laid.tile([P, 2 * (n1 - n0)], BF16, name=f"got{u}_{n0}", offset=AT_GOT + 4 * n0, align_bytes=64)
-                for n0, n1 in PARTS
-            ]
+        got = [keep.tile([P, 2 * S], F32, name=f"got{u}") for u in range(2)]
 
-        def slot(got, part, n0, n1):
-            first = PARTS[part][0]
-            return got[part][:].rearrange("p (e n) -> p e n", e=2)[:, :, n0 - first : n1 - first]
+        def gather_v(j, n0, n1):
+            at = (j % 2) * S
+            nc.vector.tensor_copy(got[j // 2][:, at + n0 : at + n1], planes[j][:].indirect(entries(n0, n1)))
 
-        def weave(copy, u, got, part, n0, n1):
+        def gather_s(j, n0, n1):
+            at = (j % 2) * S
+            nc.scalar.activation(got[j // 2][:, at + n0 : at + n1], planes[j][:].indirect(entries(n0, n1)), ACT.Copy)
+
+        def weave(copy, u, n0, n1):
             copy(
-                woven[:, PACK * n0 : PACK * n1].rearrange("p (c i j) -> p c j i", i=LINE, j=PACK)[:, :, 2 * u : 2 * u + 2, :],
-                slot(got, part, n0, n1).rearrange("p e (c i) -> p c e i", i=LINE),
+                woven[:].rearrange("p (n j) -> p n j", j=PACK)[:, n0:n1, 2 * u : 2 * u + 2],
+                got[u][:].rearrange("p (e n) -> p n e", e=2)[:, n0:n1, :],
             )
 
-        def gather_v(got, j, n0, n1):
-            nc.vector.tensor_copy(slot(got, 0, n0, n1)[:, j % 2, :], planes[j][:].indirect(entries(n0, n1)))
+        def early_plane(j):
+            gather_v(j, 0, EARLY_CUT)
+            gather_s(j, EARLY_CUT, S)
 
-        def gather_s(got, j, n0, n1):
-            nc.scalar.activation(slot(got, 1, n0, n1)[:, j % 2, :], planes[j][:].indirect(entries(n0, n1)), ACT.Copy)
-
-        def first_plane(got, j):
-            gather_v(got, j, 0, 2 * P)
-            gather_s(got, j, 2 * P, S)
-
-        def second_plane(got, j):
-            gather_v(got, j, 0, P)
-            gather_v(got, j, P, 2 * P)
-            gather_s(got, j, 2 * P, 3 * P)
-            gather_s(got, j, 3 * P, S)
-
-        got = got_tiles(0)
-        first_plane(got, 0)
+        early_plane(0)
 
         minus = keep.tile([P, HALVES], F32, name="minus")
         nc.scalar.activation(minus[:], turned[:, HALVES : 2 * HALVES], ACT.Copy, scale=-0.5)
@@ -120,28 +97,34 @@ def tile_picked_gatv_relu_e_kernel(tc, xT, w1, score, offs, pos1, pos2, out):
         for h in range(HALVES):
             nc.tensor.transpose(spread[:, h * P : (h + 1) * P], lean_cols[:, h : h + 1].to_broadcast([P, P]), ident[:])
 
-        second_plane(got, 1)
-        weave(nc.scalar.copy, 0, got, 1, 2 * P, 3 * P)
-        weave(nc.vector.tensor_copy, 0, got, 0, 0, 2 * P)
-        weave(nc.vector.tensor_copy, 0, got, 1, 3 * P, S)
-        share0 = laid.tile([P, V], F32, name="share0", offset=AT_PLANE1, align_bytes=64)
-        nc.vector.tensor_scalar(share0[:], spread[:], 0.5, 0.5, ALU.mult, ALU.add)
+        gather_v(1, 0, P)
+        gather_v(1, P, EARLY_CUT)
+        gather_s(1, EARLY_WEAVE, S)
+        gather_s(1, EARLY_CUT, EARLY_WEAVE)
+        weave(nc.scalar.copy, 0, EARLY_WEAVE, S)
+        weave(nc.vector.tensor_copy, 0, 0, P)
+        weave(nc.vector.tensor_copy, 0, P, EARLY_WEAVE)
+        share0 = keep.tile([P, V], F32, name="share0")
+        share1 = keep.tile([P, P], F32, name="share1")
+        nc.scalar.activation(share0[:], spread[:], ACT.Copy, scale=0.5, bias=0.5)
+        nc.scalar.activation(share1[:], spread[:, 0:P], ACT.Copy, scale=-0.5, bias=0.5)
 
-        got = got_tiles(1)
-        first_plane(got, 2)
-        second_plane(got, 3)
-        weave(nc.scalar.copy, 1, got, 1, 2 * P, 3 * P)
-        weave(nc.scalar.copy, 1, got, 1, 3 * P, S)
-        weave(nc.scalar.copy, 1, got, 0, CUT, 2 * P)
-        weave(nc.vector.tensor_copy, 1, got, 0, 0, P)
-        w_woven = laid.tile([P, PACK * N], BF16, name="w_woven", offset=AT_PLANE2, align_bytes=64)
+        early_plane(2)
+        gather_v(3, 0, P)
+        gather_v(3, P, 2 * P)
+        gather_s(3, 3 * P, S)
+        gather_s(3, 2 * P, 3 * P)
+        weave(nc.scalar.copy, 1, 3 * P, S)
+        weave(nc.scalar.copy, 1, 2 * P, 3 * P)
+        weave(nc.vector.tensor_copy, 1, 0, P)
+        w_woven = keep.tile([P, PACK * N], BF16, name="w_woven", align_bytes=64)
         nc.vector.tensor_copy(
             w_woven[:].rearrange("p (c i j) -> p c j i", i=LINE, j=PACK),
             w_raw[:].rearrange("p j (c i) -> p c j i", i=LINE),
         )
-        weave(nc.vector.tensor_copy, 1, got, 0, P, CUT)
+        weave(nc.vector.tensor_copy, 1, P, 2 * P)
 
-        products = [(n0, woven[:, PACK * n0 : PACK * (n0 + P)]) for n0 in (0, 2 * P, 3 * P, P)]
+        products = [(n0, woven[:, PACK * n0 : PACK * (n0 + P)]) for n0 in (0, 3 * P, P, 2 * P)]
         w_codes = keep.tile([P, N], U32, name="w_codes", align_bytes=64)
         w_scales = keep.tile([P, N], U8, name="w_scales", align_bytes=64)
         codes, scales = [], []
@@ -168,18 +151,22 @@ def tile_picked_gatv_relu_e_kernel(tc, xT, w1, score, offs, pos1, pos2, out):
 
         halves = [slice(h * P, (h + 1) * P) for h in range(HALVES)]
         term0 = keep.tile([P, V], F32, name="term0")
-        second = keep.tile([P, V], F32, name="second")
+        second = keep.tile([P, P], F32, name="second")
         term1 = keep.tile([P, V], F32, name="term1")
         total = keep.tile([P, V], F32, name="total")
         result = keep.tile([P, V], F32, name="result")
-        nc.vector.tensor_tensor(term0[:], y[:].indirect(pos1_sb[:]), share0[:], ALU.mult)
-        for cols in halves:
-            picked = y[:].indirect(pos2_sb[:, cols.start // GROUP : cols.stop // GROUP])
-            nc.scalar.activation(second[:, cols], picked, ACT.Copy)
-        for cols in halves:
-            nc.vector.scalar_tensor_tensor(term1[:, cols], spread[:, cols], 1.0, second[:, cols], ALU.subtract, ALU.mult)
-        for cols in halves:
-            nc.vector.scalar_tensor_tensor(total[:, cols], term1[:, cols], -0.5, term0[:, cols], ALU.mult, ALU.add)
+
+        def picked(pos_sb, cols):
+            return y[:].indirect(pos_sb[:, cols.start // GROUP : cols.stop // GROUP])
+
+        first, last = halves
+        nc.scalar.activation(second[:], picked(pos2_sb, last), ACT.Copy)
+        nc.vector.tensor_tensor(term0[:, first], picked(pos1_sb, first), share0[:, first], ALU.mult)
+        nc.vector.tensor_tensor(term1[:, first], picked(pos2_sb, first), share1[:], ALU.mult)
+        nc.vector.tensor_tensor(term0[:, last], picked(pos1_sb, last), share0[:, last], ALU.mult)
+        nc.vector.scalar_tensor_tensor(term1[:, last], spread[:, last], 1.0, second[:], ALU.subtract, ALU.mult)
+        nc.vector.tensor_tensor(total[:, first], term1[:, first], term0[:, first], ALU.add)
+        nc.vector.scalar_tensor_tensor(total[:, last], term1[:, last], -0.5, term0[:, last], ALU.mult, ALU.add)
         for cols in halves:
             nc.vector.tensor_scalar_max(result[:, cols], total[:, cols], 0.0)
         for cols in halves:

@@ -22,14 +22,14 @@ GROUP = 16
 HALVES = V // P
 KIB = 1024
 
-EARLY_CUT = 320
-EARLY_WEAVE = 384
+EARLY_CUT = 384
 
 
 def tile_picked_gatv_relu_e_kernel(tc, xT, w1, score, offs, pos1, pos2, out):
     nc = tc.nc
     with ExitStack() as ctx:
         keep = ctx.enter_context(tc.tile_pool(name="keep", bufs=1))
+        laid = ctx.enter_context(tc.tile_pool(name="laid", bufs=1))
         psum = ctx.enter_context(tc.psum_pool(name="psum", bufs=1))
 
         offs_sb = keep.tile([P, S // GROUP], U16, name="offs_sb")
@@ -43,7 +43,7 @@ def tile_picked_gatv_relu_e_kernel(tc, xT, w1, score, offs, pos1, pos2, out):
         nc.scalar.activation(score_rows[P // 2 :, :], zero[P // 2 :, :].to_broadcast([P // 2, P]), ACT.Copy)
 
         x_rows = xT.rearrange("(p j) t -> p j t", j=PACK)
-        planes = [keep.tile([P, T], F32, name=f"plane{j}") for j in range(PACK)]
+        planes = [laid.tile([P, T], F32, name=f"plane{j}", offset=4 * T * j, align_bytes=64) for j in range(PACK)]
         nc.sync.dma_start(out=planes[0][:], in_=x_rows[:, 0, :])
         nc.sync.dma_start(offs_sb[:], offs)
         nc.sync.dma_start(out=score_rows[0 : D * HALVES, :], in_=score[:, 0, :].rearrange("d (h c) -> d h c", c=P))
@@ -59,34 +59,7 @@ def tile_picked_gatv_relu_e_kernel(tc, xT, w1, score, offs, pos1, pos2, out):
         turned = psum.tile([P, P], F32, name="turned")
         nc.tensor.transpose(turned[:], score_rows[:], ident[:])
 
-        def entries(n0, n1):
-            return offs_sb[:, n0 // GROUP : n1 // GROUP]
-
-        woven = keep.tile([P, PACK * S], BF16, name="woven", align_bytes=64)
-
-        got = [keep.tile([P, 2 * S], F32, name=f"got{u}") for u in range(2)]
-
-        def gather_v(j, n0, n1):
-            at = (j % 2) * S
-            nc.vector.tensor_copy(got[j // 2][:, at + n0 : at + n1], planes[j][:].indirect(entries(n0, n1)))
-
-        def gather_s(j, n0, n1):
-            at = (j % 2) * S
-            nc.scalar.activation(got[j // 2][:, at + n0 : at + n1], planes[j][:].indirect(entries(n0, n1)), ACT.Copy)
-
-        def weave(copy, u, n0, n1):
-            copy(
-                woven[:].rearrange("p (n j) -> p n j", j=PACK)[:, n0:n1, 2 * u : 2 * u + 2],
-                got[u][:].rearrange("p (e n) -> p n e", e=2)[:, n0:n1, :],
-            )
-
-        def early_plane(j):
-            gather_v(j, 0, EARLY_CUT)
-            gather_s(j, EARLY_CUT, S)
-
-        early_plane(0)
-
-        minus = keep.tile([P, HALVES], F32, name="minus")
+        minus = laid.tile([P, HALVES], F32, name="minus", offset=4 * T * PACK, align_bytes=64)
         nc.scalar.activation(minus[:], turned[:, HALVES : 2 * HALVES], ACT.Copy, scale=-0.5)
         lean_cols = keep.tile([P, HALVES], F32, name="lean_cols")
         for h in range(HALVES):
@@ -97,32 +70,58 @@ def tile_picked_gatv_relu_e_kernel(tc, xT, w1, score, offs, pos1, pos2, out):
         for h in range(HALVES):
             nc.tensor.transpose(spread[:, h * P : (h + 1) * P], lean_cols[:, h : h + 1].to_broadcast([P, P]), ident[:])
 
-        gather_v(1, 0, P)
-        gather_v(1, P, EARLY_CUT)
-        gather_s(1, EARLY_WEAVE, S)
-        gather_s(1, EARLY_CUT, EARLY_WEAVE)
-        weave(nc.scalar.copy, 0, EARLY_WEAVE, S)
-        weave(nc.vector.tensor_copy, 0, 0, P)
-        weave(nc.vector.tensor_copy, 0, P, EARLY_WEAVE)
-        share0 = keep.tile([P, V], F32, name="share0")
-        share1 = keep.tile([P, P], F32, name="share1")
+        def entries(n0, n1):
+            return offs_sb[:, n0 // GROUP : n1 // GROUP]
+
+        woven = keep.tile([P, PACK * S], BF16, name="woven", align_bytes=64)
+
+        low_v = keep.tile([P, 2 * EARLY_CUT], F32, name="low_v")
+        low_s = laid.tile([P, 2 * (S - EARLY_CUT)], F32, name="low_s", offset=4 * T * PACK, align_bytes=64)
+        high = laid.tile([P, 2 * S], F32, name="high", offset=4 * T, align_bytes=64)
+
+        def slots(got, first, n0, n1):
+            return got[:].rearrange("p (e n) -> p e n", e=2)[:, :, n0 - first : n1 - first]
+
+        def gather_v(j, got, first, n0, n1):
+            nc.vector.tensor_copy(slots(got, first, n0, n1)[:, j % 2, :], planes[j][:].indirect(entries(n0, n1)))
+
+        def gather_s(j, got, first, n0, n1):
+            nc.scalar.activation(slots(got, first, n0, n1)[:, j % 2, :], planes[j][:].indirect(entries(n0, n1)), ACT.Copy)
+
+        def weave(copy, u, got, first, n0, n1):
+            copy(
+                woven[:].rearrange("p (n j) -> p n j", j=PACK)[:, n0:n1, 2 * u : 2 * u + 2],
+                slots(got, first, n0, n1).rearrange("p e n -> p n e"),
+            )
+
+        gather_v(0, low_v, 0, 0, EARLY_CUT)
+        gather_s(0, low_s, EARLY_CUT, EARLY_CUT, S)
+        gather_v(1, low_v, 0, 0, 2 * P)
+        gather_v(1, low_v, 0, 2 * P, EARLY_CUT)
+        gather_s(1, low_s, EARLY_CUT, EARLY_CUT, S)
+        weave(nc.vector.tensor_copy, 0, low_v, 0, 0, 2 * P)
+        weave(nc.vector.tensor_copy, 0, low_v, 0, 2 * P, EARLY_CUT)
+        weave(nc.scalar.copy, 0, low_s, EARLY_CUT, EARLY_CUT, S)
+
+        gather_v(2, high, 0, 0, 2 * P)
+        gather_s(2, high, 0, 2 * P, S)
+        gather_v(3, high, 0, 0, P)
+        gather_v(3, high, 0, P, 2 * P)
+        gather_s(3, high, 0, 3 * P, S)
+        gather_s(3, high, 0, 2 * P, 3 * P)
+        weave(nc.scalar.copy, 1, high, 0, 3 * P, S)
+        weave(nc.scalar.copy, 1, high, 0, 2 * P, 3 * P)
+        share0 = laid.tile([P, V], F32, name="share0", offset=4 * T * 3, align_bytes=64)
+        share1 = laid.tile([P, P], F32, name="share1", offset=4 * T * 3 + 4 * V, align_bytes=64)
         nc.scalar.activation(share0[:], spread[:], ACT.Copy, scale=0.5, bias=0.5)
         nc.scalar.activation(share1[:], spread[:, 0:P], ACT.Copy, scale=-0.5, bias=0.5)
-
-        early_plane(2)
-        gather_v(3, 0, P)
-        gather_v(3, P, 2 * P)
-        gather_s(3, 3 * P, S)
-        gather_s(3, 2 * P, 3 * P)
-        weave(nc.scalar.copy, 1, 3 * P, S)
-        weave(nc.scalar.copy, 1, 2 * P, 3 * P)
-        weave(nc.vector.tensor_copy, 1, 0, P)
-        w_woven = keep.tile([P, PACK * N], BF16, name="w_woven", align_bytes=64)
+        w_woven = laid.tile([P, PACK * N], BF16, name="w_woven", offset=4 * T * 2, align_bytes=64)
         nc.vector.tensor_copy(
             w_woven[:].rearrange("p (c i j) -> p c j i", i=LINE, j=PACK),
             w_raw[:].rearrange("p j (c i) -> p c j i", i=LINE),
         )
-        weave(nc.vector.tensor_copy, 1, P, 2 * P)
+        weave(nc.vector.tensor_copy, 1, high, 0, 0, P)
+        weave(nc.vector.tensor_copy, 1, high, 0, P, 2 * P)
 
         products = [(n0, woven[:, PACK * n0 : PACK * (n0 + P)]) for n0 in (0, 3 * P, P, 2 * P)]
         w_codes = keep.tile([P, N], U32, name="w_codes", align_bytes=64)

@@ -22,7 +22,13 @@ GROUP = 16
 HALVES = V // P
 KIB = 1024
 
-EARLY_CUT = 384
+AT_PLANE = (5 * KIB, 0, 9 * KIB, 13 * KIB)
+AT_WOVEN = 17 * KIB
+AT_SCORES = 4 * KIB
+AT_HIGH = KIB // 2
+FUSED = 64
+MID_CUT = 288
+EARLY_CUT = 320
 
 
 def tile_picked_gatv_relu_e_kernel(tc, xT, w1, score, offs, pos1, pos2, out):
@@ -36,17 +42,18 @@ def tile_picked_gatv_relu_e_kernel(tc, xT, w1, score, offs, pos1, pos2, out):
         pos1_sb = keep.tile([P, V // GROUP], U16, name="pos1_sb")
         pos2_sb = keep.tile([P, V // GROUP], U16, name="pos2_sb")
 
-        score_rows = keep.tile([P, P], F32, name="score_rows")
+        score_rows = laid.tile([P, P], F32, name="score_rows", offset=AT_SCORES, align_bytes=64)
         zero = keep.tile([P, 1], F32, name="zero")
         nc.vector.memset(zero[:], 0.0)
         nc.vector.memset(score_rows[0 : P // 2, :], 0.0)
         nc.scalar.activation(score_rows[P // 2 :, :], zero[P // 2 :, :].to_broadcast([P // 2, P]), ACT.Copy)
 
         x_rows = xT.rearrange("(p j) t -> p j t", j=PACK)
-        planes = [laid.tile([P, T], F32, name=f"plane{j}", offset=4 * T * j, align_bytes=64) for j in range(PACK)]
+        planes = [laid.tile([P, T], F32, name=f"plane{j}", offset=AT_PLANE[j], align_bytes=64) for j in range(PACK)]
         nc.sync.dma_start(out=planes[0][:], in_=x_rows[:, 0, :])
         nc.sync.dma_start(offs_sb[:], offs)
-        nc.sync.dma_start(out=score_rows[0 : D * HALVES, :], in_=score[:, 0, :].rearrange("d (h c) -> d h c", c=P))
+        score_raw = keep.tile([HALVES, D, P], F32, name="score_raw")
+        nc.sync.dma_start(out=score_raw[:], in_=score[:, 0, :].rearrange("d (h c) -> h d c", c=P))
         for j in range(1, PACK):
             nc.sync.dma_start(out=planes[j][:], in_=x_rows[:, j, :])
         w_raw = keep.tile([P, PACK, N], F32, name="w_raw")
@@ -56,28 +63,18 @@ def tile_picked_gatv_relu_e_kernel(tc, xT, w1, score, offs, pos1, pos2, out):
 
         ident = keep.tile([P, P], F32, name="ident")
         make_identity(nc, ident[:])
+        nc.gpsimd.tensor_tensor(score_rows[0:HALVES, :], score_raw[:, 0, :], score_raw[:, 1, :], ALU.subtract)
         turned = psum.tile([P, P], F32, name="turned")
         nc.tensor.transpose(turned[:], score_rows[:], ident[:])
-
-        minus = laid.tile([P, HALVES], F32, name="minus", offset=4 * T * PACK, align_bytes=64)
-        nc.scalar.activation(minus[:], turned[:, HALVES : 2 * HALVES], ACT.Copy, scale=-0.5)
-        lean_cols = keep.tile([P, HALVES], F32, name="lean_cols")
-        for h in range(HALVES):
-            nc.scalar.activation(
-                lean_cols[:, h : h + 1], turned[:, h : h + 1], ACT.Tanh, scale=0.5, bias=minus[:, h : h + 1]
-            )
-        spread = psum.tile([P, V], F32, name="spread")
-        for h in range(HALVES):
-            nc.tensor.transpose(spread[:, h * P : (h + 1) * P], lean_cols[:, h : h + 1].to_broadcast([P, P]), ident[:])
 
         def entries(n0, n1):
             return offs_sb[:, n0 // GROUP : n1 // GROUP]
 
-        woven = keep.tile([P, PACK * S], BF16, name="woven", align_bytes=64)
+        woven = laid.tile([P, PACK * S], BF16, name="woven", offset=AT_WOVEN, align_bytes=64)
 
         low_v = keep.tile([P, 2 * EARLY_CUT], F32, name="low_v")
-        low_s = laid.tile([P, 2 * (S - EARLY_CUT)], F32, name="low_s", offset=4 * T * PACK, align_bytes=64)
-        high = laid.tile([P, 2 * S], F32, name="high", offset=4 * T, align_bytes=64)
+        low_s = keep.tile([P, 2 * (S - EARLY_CUT)], F32, name="low_s")
+        high = laid.tile([P, 2 * S], F32, name="high", offset=AT_HIGH, align_bytes=64)
 
         def slots(got, first, n0, n1):
             return got[:].rearrange("p (e n) -> p e n", e=2)[:, :, n0 - first : n1 - first]
@@ -96,26 +93,27 @@ def tile_picked_gatv_relu_e_kernel(tc, xT, w1, score, offs, pos1, pos2, out):
 
         gather_v(0, low_v, 0, 0, EARLY_CUT)
         gather_s(0, low_s, EARLY_CUT, EARLY_CUT, S)
-        gather_v(1, low_v, 0, 0, 2 * P)
-        gather_v(1, low_v, 0, 2 * P, EARLY_CUT)
+        gather_v(1, low_v, 0, 0, EARLY_CUT - P)
+        gather_v(1, low_v, 0, EARLY_CUT - P, EARLY_CUT)
         gather_s(1, low_s, EARLY_CUT, EARLY_CUT, S)
-        weave(nc.vector.tensor_copy, 0, low_v, 0, 0, 2 * P)
-        weave(nc.vector.tensor_copy, 0, low_v, 0, 2 * P, EARLY_CUT)
+        lean_cols = laid.tile([P, HALVES], F32, name="lean_cols", offset=AT_PLANE[1], align_bytes=64)
+        nc.scalar.activation(lean_cols[:], turned[:, 0:HALVES], ACT.Tanh, scale=0.5)
+        spread = psum.tile([P, V], F32, name="spread")
+        for h in range(HALVES):
+            nc.tensor.transpose(spread[:, h * P : (h + 1) * P], lean_cols[:, h : h + 1].to_broadcast([P, P]), ident[:])
+        weave(nc.vector.tensor_copy, 0, low_v, 0, 0, EARLY_CUT - P)
+        weave(nc.vector.tensor_copy, 0, low_v, 0, EARLY_CUT - P, EARLY_CUT)
         weave(nc.scalar.copy, 0, low_s, EARLY_CUT, EARLY_CUT, S)
 
-        gather_v(2, high, 0, 0, 2 * P)
-        gather_s(2, high, 0, 2 * P, S)
+        gather_v(2, high, 0, 0, MID_CUT)
+        gather_s(2, high, 0, MID_CUT, S)
         gather_v(3, high, 0, 0, P)
         gather_v(3, high, 0, P, 2 * P)
         gather_s(3, high, 0, 3 * P, S)
         gather_s(3, high, 0, 2 * P, 3 * P)
         weave(nc.scalar.copy, 1, high, 0, 3 * P, S)
         weave(nc.scalar.copy, 1, high, 0, 2 * P, 3 * P)
-        share0 = laid.tile([P, V], F32, name="share0", offset=4 * T * 3, align_bytes=64)
-        share1 = laid.tile([P, P], F32, name="share1", offset=4 * T * 3 + 4 * V, align_bytes=64)
-        nc.scalar.activation(share0[:], spread[:], ACT.Copy, scale=0.5, bias=0.5)
-        nc.scalar.activation(share1[:], spread[:, 0:P], ACT.Copy, scale=-0.5, bias=0.5)
-        w_woven = laid.tile([P, PACK * N], BF16, name="w_woven", offset=4 * T * 2, align_bytes=64)
+        w_woven = laid.tile([P, PACK * N], BF16, name="w_woven", offset=AT_PLANE[2], align_bytes=64)
         nc.vector.tensor_copy(
             w_woven[:].rearrange("p (c i j) -> p c j i", i=LINE, j=PACK),
             w_raw[:].rearrange("p j (c i) -> p c j i", i=LINE),
@@ -123,20 +121,25 @@ def tile_picked_gatv_relu_e_kernel(tc, xT, w1, score, offs, pos1, pos2, out):
         weave(nc.vector.tensor_copy, 1, high, 0, 0, P)
         weave(nc.vector.tensor_copy, 1, high, 0, P, 2 * P)
 
-        products = [(n0, woven[:, PACK * n0 : PACK * (n0 + P)]) for n0 in (0, 3 * P, P, 2 * P)]
+        products = ((0, P), (3 * P, S), (P, 2 * P), (2 * P, 2 * P + P // 2), (2 * P + P // 2, 3 * P))
         w_codes = keep.tile([P, N], U32, name="w_codes", align_bytes=64)
         w_scales = keep.tile([P, N], U8, name="w_scales", align_bytes=64)
         codes, scales = [], []
-        for g, (n0, values) in enumerate(products):
-            codes.append(keep.tile([P, P], U32, name=f"codes{g}", align_bytes=64))
-            scales.append(keep.tile([P, P], U8, name=f"scales{g}", align_bytes=64))
-            nc.vector.quantize_mx(out=codes[g][:].bitcast(FP8X4), scales=scales[g][:], in_=values)
+        for g, (n0, n1) in enumerate(products):
+            codes.append(keep.tile([P, n1 - n0], U32, name=f"codes{g}", align_bytes=64))
+            scales.append(keep.tile([P, n1 - n0], U8, name=f"scales{g}", align_bytes=64))
+            nc.vector.quantize_mx(out=codes[g][:].bitcast(FP8X4), scales=scales[g][:], in_=woven[:, PACK * n0 : PACK * n1])
             if g == 0:
                 nc.vector.quantize_mx(out=w_codes[:].bitcast(FP8X4), scales=w_scales[:], in_=w_woven[:])
 
+        share0 = laid.tile([P, V], F32, name="share0", offset=AT_WOVEN, align_bytes=64)
+        share1 = laid.tile([P, FUSED], F32, name="share1", offset=AT_WOVEN + 4 * V, align_bytes=64)
+        nc.vector.tensor_scalar(share0[:], spread[:], 0.5, 0.5, ALU.mult, ALU.add)
+        nc.vector.tensor_scalar_add(share1[:], spread[:, 0:FUSED], -1.0)
+
         y = keep.tile([P, S], F32, name="y")
-        for g, (n0, values) in enumerate(products):
-            acc = psum.tile([P, P], F32, name=f"acc{g}")
+        for g, (n0, n1) in enumerate(products):
+            acc = psum.tile([P, n1 - n0], F32, name=f"acc{g}")
             nc.tensor.matmul_mx(
                 out=acc[:],
                 lhsT=w_codes[:].bitcast(FP8X4),
@@ -146,11 +149,11 @@ def tile_picked_gatv_relu_e_kernel(tc, xT, w1, score, offs, pos1, pos2, out):
                 start=True,
                 stop=True,
             )
-            nc.scalar.copy(y[:, n0 : n0 + P], acc[:])
+            nc.scalar.copy(y[:, n0:n1], acc[:])
 
         halves = [slice(h * P, (h + 1) * P) for h in range(HALVES)]
         term0 = keep.tile([P, V], F32, name="term0")
-        second = keep.tile([P, P], F32, name="second")
+        second = keep.tile([P, V], F32, name="second")
         term1 = keep.tile([P, V], F32, name="term1")
         total = keep.tile([P, V], F32, name="total")
         result = keep.tile([P, V], F32, name="result")
@@ -158,14 +161,14 @@ def tile_picked_gatv_relu_e_kernel(tc, xT, w1, score, offs, pos1, pos2, out):
         def picked(pos_sb, cols):
             return y[:].indirect(pos_sb[:, cols.start // GROUP : cols.stop // GROUP])
 
-        first, last = halves
-        nc.scalar.activation(second[:], picked(pos2_sb, last), ACT.Copy)
-        nc.vector.tensor_tensor(term0[:, first], picked(pos1_sb, first), share0[:, first], ALU.mult)
-        nc.vector.tensor_tensor(term1[:, first], picked(pos2_sb, first), share1[:], ALU.mult)
-        nc.vector.tensor_tensor(term0[:, last], picked(pos1_sb, last), share0[:, last], ALU.mult)
-        nc.vector.scalar_tensor_tensor(term1[:, last], spread[:, last], 1.0, second[:], ALU.subtract, ALU.mult)
-        nc.vector.tensor_tensor(total[:, first], term1[:, first], term0[:, first], ALU.add)
-        nc.vector.scalar_tensor_tensor(total[:, last], term1[:, last], -0.5, term0[:, last], ALU.mult, ALU.add)
+        fused, plain = slice(0, FUSED), slice(FUSED, V)
+        nc.scalar.activation(second[:, plain], picked(pos2_sb, plain), ACT.Copy)
+        nc.vector.tensor_tensor(term0[:], y[:].indirect(pos1_sb[:]), share0[:], ALU.mult)
+        nc.vector.tensor_tensor(term1[:, fused], picked(pos2_sb, fused), share1[:], ALU.mult)
+        for cols in (slice(FUSED, P), slice(P, V)):
+            nc.vector.scalar_tensor_tensor(term1[:, cols], spread[:, cols], 1.0, second[:, cols], ALU.subtract, ALU.mult)
+        for cols in halves:
+            nc.vector.scalar_tensor_tensor(total[:, cols], term1[:, cols], -0.5, term0[:, cols], ALU.mult, ALU.add)
         for cols in halves:
             nc.vector.tensor_scalar_max(result[:, cols], total[:, cols], 0.0)
         for cols in halves:

@@ -27,7 +27,7 @@ AT_WOVEN = 17 * KIB
 AT_SCORES = 4 * KIB
 AT_HIGH = KIB // 2
 FUSED = 64
-MID_CUT = 288
+MID_CUT = 352
 EARLY_CUT = 320
 
 
@@ -113,15 +113,15 @@ def tile_picked_gatv_relu_e_kernel(tc, xT, w1, score, offs, pos1, pos2, out):
         gather_s(3, high, 0, 2 * P, 3 * P)
         weave(nc.scalar.copy, 1, high, 0, 3 * P, S)
         weave(nc.scalar.copy, 1, high, 0, 2 * P, 3 * P)
+        weave(nc.vector.tensor_copy, 1, high, 0, 0, P)
         w_woven = laid.tile([P, PACK * N], BF16, name="w_woven", offset=AT_PLANE[2], align_bytes=64)
         nc.vector.tensor_copy(
             w_woven[:].rearrange("p (c i j) -> p c j i", i=LINE, j=PACK),
             w_raw[:].rearrange("p j (c i) -> p c j i", i=LINE),
         )
-        weave(nc.vector.tensor_copy, 1, high, 0, 0, P)
         weave(nc.vector.tensor_copy, 1, high, 0, P, 2 * P)
 
-        products = ((0, P), (3 * P, S), (P, 2 * P), (2 * P, 2 * P + P // 2), (2 * P + P // 2, 3 * P))
+        products = ((0, P), (3 * P, S), (P, 2 * P), (2 * P, 3 * P))
         w_codes = keep.tile([P, N], U32, name="w_codes", align_bytes=64)
         w_scales = keep.tile([P, N], U8, name="w_scales", align_bytes=64)
         codes, scales = [], []

@@ -22,13 +22,14 @@ GROUP = 16
 HALVES = V // P
 KIB = 1024
 
+LOW_CUT = 320
+LOW_MID = 416
+MID_CUT = 320
+FUSED = 64
+
 AT_PLANE = (5 * KIB, 0, 9 * KIB, 13 * KIB)
-AT_WOVEN = 17 * KIB
 AT_SCORES = 4 * KIB
 AT_HIGH = KIB // 2
-FUSED = 64
-MID_CUT = 352
-EARLY_CUT = 320
 
 
 def tile_picked_gatv_relu_e_kernel(tc, xT, w1, score, offs, pos1, pos2, out):
@@ -67,79 +68,86 @@ def tile_picked_gatv_relu_e_kernel(tc, xT, w1, score, offs, pos1, pos2, out):
         turned = psum.tile([P, P], F32, name="turned")
         nc.tensor.transpose(turned[:], score_rows[:], ident[:])
 
-        def entries(n0, n1):
-            return offs_sb[:, n0 // GROUP : n1 // GROUP]
-
-        woven = laid.tile([P, PACK * S], BF16, name="woven", offset=AT_WOVEN, align_bytes=64)
-
-        low_v = keep.tile([P, 2 * EARLY_CUT], F32, name="low_v")
-        low_s = keep.tile([P, 2 * (S - EARLY_CUT)], F32, name="low_s")
+        woven = keep.tile([P, PACK * S], BF16, name="woven", align_bytes=64)
+        low_v = keep.tile([P, 2 * LOW_CUT], F32, name="low_v")
+        low_s = keep.tile([P, 2 * (S - LOW_CUT)], F32, name="low_s")
         high = laid.tile([P, 2 * S], F32, name="high", offset=AT_HIGH, align_bytes=64)
 
-        def slots(got, first, n0, n1):
-            return got[:].rearrange("p (e n) -> p e n", e=2)[:, :, n0 - first : n1 - first]
+        def both_planes(gathered, first, n0, n1):
+            return gathered[:].rearrange("p (e n) -> p e n", e=2)[:, :, n0 - first : n1 - first]
 
-        def gather_v(j, got, first, n0, n1):
-            nc.vector.tensor_copy(slots(got, first, n0, n1)[:, j % 2, :], planes[j][:].indirect(entries(n0, n1)))
+        def picked_nodes(j, n0, n1):
+            return planes[j][:].indirect(offs_sb[:, n0 // GROUP : n1 // GROUP])
 
-        def gather_s(j, got, first, n0, n1):
-            nc.scalar.activation(slots(got, first, n0, n1)[:, j % 2, :], planes[j][:].indirect(entries(n0, n1)), ACT.Copy)
+        def gather_v(j, gathered, first, n0, n1):
+            nc.vector.tensor_copy(both_planes(gathered, first, n0, n1)[:, j % 2, :], picked_nodes(j, n0, n1))
 
-        def weave(copy, u, got, first, n0, n1):
+        def gather_s(j, gathered, first, n0, n1):
+            nc.scalar.activation(both_planes(gathered, first, n0, n1)[:, j % 2, :], picked_nodes(j, n0, n1), ACT.Copy)
+
+        def weave(copy, j, gathered, first, n0, n1):
             copy(
-                woven[:].rearrange("p (n j) -> p n j", j=PACK)[:, n0:n1, 2 * u : 2 * u + 2],
-                slots(got, first, n0, n1).rearrange("p e n -> p n e"),
+                woven[:].rearrange("p (n j) -> p n j", j=PACK)[:, n0:n1, j : j + 2],
+                both_planes(gathered, first, n0, n1).rearrange("p e n -> p n e"),
             )
 
-        gather_v(0, low_v, 0, 0, EARLY_CUT)
-        gather_s(0, low_s, EARLY_CUT, EARLY_CUT, S)
-        gather_v(1, low_v, 0, 0, EARLY_CUT - P)
-        gather_v(1, low_v, 0, EARLY_CUT - P, EARLY_CUT)
-        gather_s(1, low_s, EARLY_CUT, EARLY_CUT, S)
+        gather_v(0, low_v, 0, 0, LOW_CUT)
+        gather_s(0, low_s, LOW_CUT, LOW_CUT, S)
+        pieces_v = ((0, LOW_CUT - P), (LOW_CUT - P, LOW_CUT))
+        pieces_s = ((LOW_CUT, LOW_MID), (LOW_MID, S))
+        for n0, n1 in pieces_v:
+            gather_v(1, low_v, 0, n0, n1)
+        for n0, n1 in pieces_s:
+            gather_s(1, low_s, LOW_CUT, n0, n1)
+
         lean_cols = laid.tile([P, HALVES], F32, name="lean_cols", offset=AT_PLANE[1], align_bytes=64)
         nc.scalar.activation(lean_cols[:], turned[:, 0:HALVES], ACT.Tanh, scale=0.5)
         spread = psum.tile([P, V], F32, name="spread")
         for h in range(HALVES):
             nc.tensor.transpose(spread[:, h * P : (h + 1) * P], lean_cols[:, h : h + 1].to_broadcast([P, P]), ident[:])
-        weave(nc.vector.tensor_copy, 0, low_v, 0, 0, EARLY_CUT - P)
-        weave(nc.vector.tensor_copy, 0, low_v, 0, EARLY_CUT - P, EARLY_CUT)
-        weave(nc.scalar.copy, 0, low_s, EARLY_CUT, EARLY_CUT, S)
+
+        for n0, n1 in pieces_v:
+            weave(nc.vector.tensor_copy, 0, low_v, 0, n0, n1)
+        for n0, n1 in pieces_s:
+            weave(nc.scalar.copy, 0, low_s, LOW_CUT, n0, n1)
 
         gather_v(2, high, 0, 0, MID_CUT)
         gather_s(2, high, 0, MID_CUT, S)
-        gather_v(3, high, 0, 0, P)
-        gather_v(3, high, 0, P, 2 * P)
-        gather_s(3, high, 0, 3 * P, S)
-        gather_s(3, high, 0, 2 * P, 3 * P)
-        weave(nc.scalar.copy, 1, high, 0, 3 * P, S)
-        weave(nc.scalar.copy, 1, high, 0, 2 * P, 3 * P)
-        weave(nc.vector.tensor_copy, 1, high, 0, 0, P)
+        for n0 in (0, P):
+            gather_v(3, high, 0, n0, n0 + P)
+        for n0 in (3 * P, 2 * P):
+            gather_s(3, high, 0, n0, n0 + P)
+        for n0 in (3 * P, 2 * P):
+            weave(nc.scalar.copy, 2, high, 0, n0, n0 + P)
+
+        share0 = laid.tile([P, V], F32, name="share0", offset=AT_PLANE[3], align_bytes=64)
+        less1 = laid.tile([P, FUSED], F32, name="less1", offset=AT_PLANE[3] + 4 * V, align_bytes=64)
+        nc.scalar.activation(share0[:], spread[:], ACT.Copy, scale=0.5, bias=0.5)
+        nc.scalar.activation(less1[:], spread[:, 0:FUSED], ACT.Copy, bias=-1.0)
+
+        weave(nc.vector.tensor_copy, 2, high, 0, 0, P)
         w_woven = laid.tile([P, PACK * N], BF16, name="w_woven", offset=AT_PLANE[2], align_bytes=64)
         nc.vector.tensor_copy(
             w_woven[:].rearrange("p (c i j) -> p c j i", i=LINE, j=PACK),
             w_raw[:].rearrange("p j (c i) -> p c j i", i=LINE),
         )
-        weave(nc.vector.tensor_copy, 1, high, 0, P, 2 * P)
+        weave(nc.vector.tensor_copy, 2, high, 0, P, 2 * P)
 
-        products = ((0, P), (3 * P, S), (P, 2 * P), (2 * P, 3 * P))
+        products = (0, 3 * P, P, 2 * P)
         w_codes = keep.tile([P, N], U32, name="w_codes", align_bytes=64)
         w_scales = keep.tile([P, N], U8, name="w_scales", align_bytes=64)
         codes, scales = [], []
-        for g, (n0, n1) in enumerate(products):
-            codes.append(keep.tile([P, n1 - n0], U32, name=f"codes{g}", align_bytes=64))
-            scales.append(keep.tile([P, n1 - n0], U8, name=f"scales{g}", align_bytes=64))
-            nc.vector.quantize_mx(out=codes[g][:].bitcast(FP8X4), scales=scales[g][:], in_=woven[:, PACK * n0 : PACK * n1])
+        for g, n0 in enumerate(products):
+            codes.append(keep.tile([P, P], U32, name=f"codes{g}", align_bytes=64))
+            scales.append(keep.tile([P, P], U8, name=f"scales{g}", align_bytes=64))
+            values = woven[:, PACK * n0 : PACK * (n0 + P)]
+            nc.vector.quantize_mx(out=codes[g][:].bitcast(FP8X4), scales=scales[g][:], in_=values)
             if g == 0:
                 nc.vector.quantize_mx(out=w_codes[:].bitcast(FP8X4), scales=w_scales[:], in_=w_woven[:])
 
-        share0 = laid.tile([P, V], F32, name="share0", offset=AT_WOVEN, align_bytes=64)
-        share1 = laid.tile([P, FUSED], F32, name="share1", offset=AT_WOVEN + 4 * V, align_bytes=64)
-        nc.vector.tensor_scalar(share0[:], spread[:], 0.5, 0.5, ALU.mult, ALU.add)
-        nc.vector.tensor_scalar_add(share1[:], spread[:, 0:FUSED], -1.0)
-
         y = keep.tile([P, S], F32, name="y")
-        for g, (n0, n1) in enumerate(products):
-            acc = psum.tile([P, n1 - n0], F32, name=f"acc{g}")
+        for g, n0 in enumerate(products):
+            acc = psum.tile([P, P], F32, name=f"acc{g}")
             nc.tensor.matmul_mx(
                 out=acc[:],
                 lhsT=w_codes[:].bitcast(FP8X4),
@@ -149,7 +157,7 @@ def tile_picked_gatv_relu_e_kernel(tc, xT, w1, score, offs, pos1, pos2, out):
                 start=True,
                 stop=True,
             )
-            nc.scalar.copy(y[:, n0:n1], acc[:])
+            nc.scalar.copy(y[:, n0 : n0 + P], acc[:])
 
         halves = [slice(h * P, (h + 1) * P) for h in range(HALVES)]
         term0 = keep.tile([P, V], F32, name="term0")
@@ -158,13 +166,13 @@ def tile_picked_gatv_relu_e_kernel(tc, xT, w1, score, offs, pos1, pos2, out):
         total = keep.tile([P, V], F32, name="total")
         result = keep.tile([P, V], F32, name="result")
 
-        def picked(pos_sb, cols):
-            return y[:].indirect(pos_sb[:, cols.start // GROUP : cols.stop // GROUP])
+        def second_neighbours(cols):
+            return y[:].indirect(pos2_sb[:, cols.start // GROUP : cols.stop // GROUP])
 
         fused, plain = slice(0, FUSED), slice(FUSED, V)
-        nc.scalar.activation(second[:, plain], picked(pos2_sb, plain), ACT.Copy)
+        nc.scalar.activation(second[:, plain], second_neighbours(plain), ACT.Copy)
         nc.vector.tensor_tensor(term0[:], y[:].indirect(pos1_sb[:]), share0[:], ALU.mult)
-        nc.vector.tensor_tensor(term1[:, fused], picked(pos2_sb, fused), share1[:], ALU.mult)
+        nc.vector.tensor_tensor(term1[:, fused], second_neighbours(fused), less1[:], ALU.mult)
         for cols in (slice(FUSED, P), slice(P, V)):
             nc.vector.scalar_tensor_tensor(term1[:, cols], spread[:, cols], 1.0, second[:, cols], ALU.subtract, ALU.mult)
         for cols in halves:

@@ -54,7 +54,7 @@ def tile_picked_gatv_relu_e_kernel(tc, xT, w1, score, offs, pos1, pos2, out):
         nc.sync.dma_start(out=planes[0][:], in_=x_rows[:, 0, :])
         nc.sync.dma_start(offs_sb[:], offs)
         score_raw = keep.tile([HALVES, D, P], F32, name="score_raw")
-        nc.sync.dma_start(out=score_raw[:], in_=score[:, 0, :].rearrange("d (h c) -> h d c", c=P))
+        nc.scalar.dma_start(out=score_raw[:], in_=score[:, 0, :].rearrange("d (h c) -> h d c", c=P))
         for j in range(1, PACK):
             nc.sync.dma_start(out=planes[j][:], in_=x_rows[:, j, :])
         w_raw = keep.tile([P, PACK, N], F32, name="w_raw")

@@ -27,6 +27,8 @@ LOW_MID = 416
 MID_CUT = 320
 FUSED = 64
 
+LAST = 160
+
 AT_PLANE = (5 * KIB, 0, 9 * KIB, 13 * KIB)
 AT_SCORES = 4 * KIB
 AT_HIGH = KIB // 2
@@ -133,21 +135,21 @@ def tile_picked_gatv_relu_e_kernel(tc, xT, w1, score, offs, pos1, pos2, out):
         )
         weave(nc.vector.tensor_copy, 2, high, 0, P, 2 * P)
 
-        products = (0, 3 * P, P, 2 * P)
+        products = ((0, P), (3 * P, S), (P, 2 * P), (2 * P, 3 * P))
         w_codes = keep.tile([P, N], U32, name="w_codes", align_bytes=64)
         w_scales = keep.tile([P, N], U8, name="w_scales", align_bytes=64)
         codes, scales = [], []
-        for g, n0 in enumerate(products):
-            codes.append(keep.tile([P, P], U32, name=f"codes{g}", align_bytes=64))
-            scales.append(keep.tile([P, P], U8, name=f"scales{g}", align_bytes=64))
-            values = woven[:, PACK * n0 : PACK * (n0 + P)]
+        for g, (n0, n1) in enumerate(products):
+            codes.append(keep.tile([P, n1 - n0], U32, name=f"codes{g}", align_bytes=64))
+            scales.append(keep.tile([P, n1 - n0], U8, name=f"scales{g}", align_bytes=64))
+            values = woven[:, PACK * n0 : PACK * n1]
             nc.vector.quantize_mx(out=codes[g][:].bitcast(FP8X4), scales=scales[g][:], in_=values)
             if g == 0:
                 nc.vector.quantize_mx(out=w_codes[:].bitcast(FP8X4), scales=w_scales[:], in_=w_woven[:])
 
         y = keep.tile([P, S], F32, name="y")
-        for g, n0 in enumerate(products):
-            acc = psum.tile([P, P], F32, name=f"acc{g}")
+        for g, (n0, n1) in enumerate(products):
+            acc = psum.tile([P, n1 - n0], F32, name=f"acc{g}")
             nc.tensor.matmul_mx(
                 out=acc[:],
                 lhsT=w_codes[:].bitcast(FP8X4),
@@ -157,9 +159,8 @@ def tile_picked_gatv_relu_e_kernel(tc, xT, w1, score, offs, pos1, pos2, out):
                 start=True,
                 stop=True,
             )
-            nc.scalar.copy(y[:, n0 : n0 + P], acc[:])
+            nc.scalar.copy(y[:, n0:n1], acc[:])
 
-        halves = [slice(h * P, (h + 1) * P) for h in range(HALVES)]
         term0 = keep.tile([P, V], F32, name="term0")
         second = keep.tile([P, V], F32, name="second")
         term1 = keep.tile([P, V], F32, name="term1")
@@ -169,15 +170,16 @@ def tile_picked_gatv_relu_e_kernel(tc, xT, w1, score, offs, pos1, pos2, out):
         def second_neighbours(cols):
             return y[:].indirect(pos2_sb[:, cols.start // GROUP : cols.stop // GROUP])
 
-        fused, plain = slice(0, FUSED), slice(FUSED, V)
-        nc.scalar.activation(second[:, plain], second_neighbours(plain), ACT.Copy)
+        fused, plain = slice(0, FUSED), (slice(FUSED, LAST), slice(LAST, V))
+        for cols in plain:
+            nc.scalar.activation(second[:, cols], second_neighbours(cols), ACT.Copy)
         nc.vector.tensor_tensor(term0[:], y[:].indirect(pos1_sb[:]), share0[:], ALU.mult)
         nc.vector.tensor_tensor(term1[:, fused], second_neighbours(fused), less1[:], ALU.mult)
-        for cols in (slice(FUSED, P), slice(P, V)):
+        for cols in plain:
             nc.vector.scalar_tensor_tensor(term1[:, cols], spread[:, cols], 1.0, second[:, cols], ALU.subtract, ALU.mult)
-        for cols in halves:
+        for cols in (fused, *plain):
             nc.vector.scalar_tensor_tensor(total[:, cols], term1[:, cols], -0.5, term0[:, cols], ALU.mult, ALU.add)
-        for cols in halves:
+        for cols in (fused, *plain):
             nc.vector.tensor_scalar_max(result[:, cols], total[:, cols], 0.0)
-        for cols in halves:
+        for cols in (slice(0, LAST), slice(LAST, V)):
             nc.sync.dma_start(out=out[:, cols], in_=result[:, cols])

@@ -27,8 +27,6 @@ LOW_MID = 416
 MID_CUT = 320
 FUSED = 64
 
-LAST = 160
-
 AT_PLANE = (5 * KIB, 0, 9 * KIB, 13 * KIB)
 AT_SCORES = 4 * KIB
 AT_HIGH = KIB // 2
@@ -115,8 +113,7 @@ def tile_picked_gatv_relu_e_kernel(tc, xT, w1, score, offs, pos1, pos2, out):
 
         gather_v(2, high, 0, 0, MID_CUT)
         gather_s(2, high, 0, MID_CUT, S)
-        for n0 in (0, P):
-            gather_v(3, high, 0, n0, n0 + P)
+        gather_v(3, high, 0, 0, 2 * P)
         for n0 in (3 * P, 2 * P):
             gather_s(3, high, 0, n0, n0 + P)
         for n0 in (3 * P, 2 * P):
@@ -127,25 +124,23 @@ def tile_picked_gatv_relu_e_kernel(tc, xT, w1, score, offs, pos1, pos2, out):
         nc.scalar.activation(share0[:], spread[:], ACT.Copy, scale=0.5, bias=0.5)
         nc.scalar.activation(less1[:], spread[:, 0:FUSED], ACT.Copy, bias=-1.0)
 
-        weave(nc.vector.tensor_copy, 2, high, 0, 0, P)
         w_woven = laid.tile([P, PACK * N], BF16, name="w_woven", offset=AT_PLANE[2], align_bytes=64)
         nc.vector.tensor_copy(
             w_woven[:].rearrange("p (c i j) -> p c j i", i=LINE, j=PACK),
             w_raw[:].rearrange("p j (c i) -> p c j i", i=LINE),
         )
-        weave(nc.vector.tensor_copy, 2, high, 0, P, 2 * P)
+        weave(nc.vector.tensor_copy, 2, high, 0, 0, 2 * P)
 
-        products = ((0, P), (3 * P, S), (P, 2 * P), (2 * P, 3 * P))
+        products = ((3 * P, S), (0, P), (P, 2 * P), (2 * P, 3 * P))
         w_codes = keep.tile([P, N], U32, name="w_codes", align_bytes=64)
         w_scales = keep.tile([P, N], U8, name="w_scales", align_bytes=64)
+        nc.vector.quantize_mx(out=w_codes[:].bitcast(FP8X4), scales=w_scales[:], in_=w_woven[:])
         codes, scales = [], []
         for g, (n0, n1) in enumerate(products):
             codes.append(keep.tile([P, n1 - n0], U32, name=f"codes{g}", align_bytes=64))
             scales.append(keep.tile([P, n1 - n0], U8, name=f"scales{g}", align_bytes=64))
             values = woven[:, PACK * n0 : PACK * n1]
             nc.vector.quantize_mx(out=codes[g][:].bitcast(FP8X4), scales=scales[g][:], in_=values)
-            if g == 0:
-                nc.vector.quantize_mx(out=w_codes[:].bitcast(FP8X4), scales=w_scales[:], in_=w_woven[:])
 
         y = keep.tile([P, S], F32, name="y")
         for g, (n0, n1) in enumerate(products):
@@ -161,6 +156,7 @@ def tile_picked_gatv_relu_e_kernel(tc, xT, w1, score, offs, pos1, pos2, out):
             )
             nc.scalar.copy(y[:, n0:n1], acc[:])
 
+        halves = [slice(h * P, (h + 1) * P) for h in range(HALVES)]
         term0 = keep.tile([P, V], F32, name="term0")
         second = keep.tile([P, V], F32, name="second")
         term1 = keep.tile([P, V], F32, name="term1")
@@ -170,16 +166,15 @@ def tile_picked_gatv_relu_e_kernel(tc, xT, w1, score, offs, pos1, pos2, out):
         def second_neighbours(cols):
             return y[:].indirect(pos2_sb[:, cols.start // GROUP : cols.stop // GROUP])
 
-        fused, plain = slice(0, FUSED), (slice(FUSED, LAST), slice(LAST, V))
-        for cols in plain:
-            nc.scalar.activation(second[:, cols], second_neighbours(cols), ACT.Copy)
+        fused, plain = slice(0, FUSED), slice(FUSED, V)
+        nc.scalar.activation(second[:, plain], second_neighbours(plain), ACT.Copy)
         nc.vector.tensor_tensor(term0[:], y[:].indirect(pos1_sb[:]), share0[:], ALU.mult)
         nc.vector.tensor_tensor(term1[:, fused], second_neighbours(fused), less1[:], ALU.mult)
-        for cols in plain:
+        for cols in (slice(FUSED, P), slice(P, V)):
             nc.vector.scalar_tensor_tensor(term1[:, cols], spread[:, cols], 1.0, second[:, cols], ALU.subtract, ALU.mult)
-        for cols in (fused, *plain):
+        for cols in halves:
             nc.vector.scalar_tensor_tensor(total[:, cols], term1[:, cols], -0.5, term0[:, cols], ALU.mult, ALU.add)
-        for cols in (fused, *plain):
+        for cols in halves:
             nc.vector.tensor_scalar_max(result[:, cols], total[:, cols], 0.0)
-        for cols in (slice(0, LAST), slice(LAST, V)):
+        for cols in halves:
             nc.sync.dma_start(out=out[:, cols], in_=result[:, cols])

@@ -1,3 +1,4 @@
+import math
 from contextlib import ExitStack
 
 import concourse.mybir as mybir
@@ -25,9 +26,14 @@ KIB = 1024
 LOW_CUT = 320
 LOW_MID = 416
 MID_CUT = 320
-FUSED = 64
+SPLIT = 128
+
+SMALL = 2.0**-32
+CAP = -math.log(SMALL)
 
 AT_PLANE = (5 * KIB, 0, 9 * KIB, 13 * KIB)
+AT_WOVEN = 17 * KIB
+AT_Y = 21 * KIB
 AT_SCORES = 4 * KIB
 AT_HIGH = KIB // 2
 
@@ -64,11 +70,13 @@ def tile_picked_gatv_relu_e_kernel(tc, xT, w1, score, offs, pos1, pos2, out):
 
         ident = keep.tile([P, P], F32, name="ident")
         make_identity(nc, ident[:])
-        nc.gpsimd.tensor_tensor(score_rows[0:HALVES, :], score_raw[:, 0, :], score_raw[:, 1, :], ALU.subtract)
+        gap = keep.tile([HALVES, P], F32, name="gap")
+        nc.gpsimd.tensor_tensor(gap[:], score_raw[:, 1, :], score_raw[:, 0, :], ALU.subtract)
+        nc.gpsimd.tensor_scalar_min(score_rows[0:HALVES, :], gap[:], CAP)
         turned = psum.tile([P, P], F32, name="turned")
         nc.tensor.transpose(turned[:], score_rows[:], ident[:])
 
-        woven = keep.tile([P, PACK * S], BF16, name="woven", align_bytes=64)
+        woven = laid.tile([P, PACK * S], BF16, name="woven", offset=AT_WOVEN, align_bytes=64)
         low_v = keep.tile([P, 2 * LOW_CUT], F32, name="low_v")
         low_s = keep.tile([P, 2 * (S - LOW_CUT)], F32, name="low_s")
         high = laid.tile([P, 2 * S], F32, name="high", offset=AT_HIGH, align_bytes=64)
@@ -100,11 +108,17 @@ def tile_picked_gatv_relu_e_kernel(tc, xT, w1, score, offs, pos1, pos2, out):
         for n0, n1 in pieces_s:
             gather_s(1, low_s, LOW_CUT, n0, n1)
 
-        lean_cols = laid.tile([P, HALVES], F32, name="lean_cols", offset=AT_PLANE[1], align_bytes=64)
-        nc.scalar.activation(lean_cols[:], turned[:, 0:HALVES], ACT.Tanh, scale=0.5)
-        spread = psum.tile([P, V], F32, name="spread")
-        for h in range(HALVES):
-            nc.tensor.transpose(spread[:, h * P : (h + 1) * P], lean_cols[:, h : h + 1].to_broadcast([P, P]), ident[:])
+        def spread(cols, name):
+            rows = psum.tile([P, V], F32, name=name)
+            for h in range(HALVES):
+                nc.tensor.transpose(rows[:, h * P : (h + 1) * P], cols[:, h : h + 1].to_broadcast([P, P]), ident[:])
+            return rows
+
+        odds_cols = laid.tile([P, HALVES], F32, name="odds_cols", offset=AT_PLANE[1], align_bytes=64)
+        nc.scalar.activation(odds_cols[:], turned[:, 0:HALVES], ACT.Exp)
+        odds = spread(odds_cols, "odds")
+        whole_cols = keep.tile([P, HALVES], F32, name="whole_cols")
+        nc.gpsimd.tensor_scalar(whole_cols[:], odds_cols[:], SMALL, SMALL, ALU.mult, ALU.add)
 
         for n0, n1 in pieces_v:
             weave(nc.vector.tensor_copy, 0, low_v, 0, n0, n1)
@@ -119,10 +133,8 @@ def tile_picked_gatv_relu_e_kernel(tc, xT, w1, score, offs, pos1, pos2, out):
         for n0 in (3 * P, 2 * P):
             weave(nc.scalar.copy, 2, high, 0, n0, n0 + P)
 
-        share0 = laid.tile([P, V], F32, name="share0", offset=AT_PLANE[3], align_bytes=64)
-        less1 = laid.tile([P, FUSED], F32, name="less1", offset=AT_PLANE[3] + 4 * V, align_bytes=64)
-        nc.scalar.activation(share0[:], spread[:], ACT.Copy, scale=0.5, bias=0.5)
-        nc.scalar.activation(less1[:], spread[:, 0:FUSED], ACT.Copy, bias=-1.0)
+        weight1 = laid.tile([P, V], F32, name="weight1", offset=AT_PLANE[3], align_bytes=64)
+        nc.scalar.activation(weight1[:], odds[:], ACT.Copy, scale=SMALL)
 
         w_woven = laid.tile([P, PACK * N], BF16, name="w_woven", offset=AT_PLANE[2], align_bytes=64)
         nc.vector.tensor_copy(
@@ -142,7 +154,10 @@ def tile_picked_gatv_relu_e_kernel(tc, xT, w1, score, offs, pos1, pos2, out):
             values = woven[:, PACK * n0 : PACK * n1]
             nc.vector.quantize_mx(out=codes[g][:].bitcast(FP8X4), scales=scales[g][:], in_=values)
 
-        y = keep.tile([P, S], F32, name="y")
+        norm_cols = laid.tile([P, HALVES], F32, name="norm_cols", offset=AT_WOVEN, align_bytes=64)
+        nc.vector.reciprocal(norm_cols[:], whole_cols[:])
+
+        y = laid.tile([P, S], F32, name="y", offset=AT_Y, align_bytes=64)
         for g, (n0, n1) in enumerate(products):
             acc = psum.tile([P, n1 - n0], F32, name=f"acc{g}")
             nc.tensor.matmul_mx(
@@ -156,25 +171,22 @@ def tile_picked_gatv_relu_e_kernel(tc, xT, w1, score, offs, pos1, pos2, out):
             )
             nc.scalar.copy(y[:, n0:n1], acc[:])
 
-        halves = [slice(h * P, (h + 1) * P) for h in range(HALVES)]
-        term0 = keep.tile([P, V], F32, name="term0")
-        second = keep.tile([P, V], F32, name="second")
+        norm = spread(norm_cols, "norm")
+        pieces = (slice(0, SPLIT), slice(SPLIT, V))
+        first = keep.tile([P, V], F32, name="first")
         term1 = keep.tile([P, V], F32, name="term1")
         total = keep.tile([P, V], F32, name="total")
-        result = keep.tile([P, V], F32, name="result")
+        result = laid.tile([P, V], F32, name="result", offset=AT_Y, align_bytes=64)
 
-        def second_neighbours(cols):
-            return y[:].indirect(pos2_sb[:, cols.start // GROUP : cols.stop // GROUP])
+        def neighbours(places, cols):
+            return y[:].indirect(places[:, cols.start // GROUP : cols.stop // GROUP])
 
-        fused, plain = slice(0, FUSED), slice(FUSED, V)
-        nc.scalar.activation(second[:, plain], second_neighbours(plain), ACT.Copy)
-        nc.vector.tensor_tensor(term0[:], y[:].indirect(pos1_sb[:]), share0[:], ALU.mult)
-        nc.vector.tensor_tensor(term1[:, fused], second_neighbours(fused), less1[:], ALU.mult)
-        for cols in (slice(FUSED, P), slice(P, V)):
-            nc.vector.scalar_tensor_tensor(term1[:, cols], spread[:, cols], 1.0, second[:, cols], ALU.subtract, ALU.mult)
-        for cols in halves:
-            nc.vector.scalar_tensor_tensor(total[:, cols], term1[:, cols], -0.5, term0[:, cols], ALU.mult, ALU.add)
-        for cols in halves:
-            nc.vector.tensor_scalar_max(result[:, cols], total[:, cols], 0.0)
-        for cols in halves:
+        for cols in pieces:
+            nc.scalar.activation(first[:, cols], neighbours(pos1_sb, cols), ACT.Copy)
+            nc.vector.tensor_tensor(term1[:, cols], neighbours(pos2_sb, cols), weight1[:, cols], ALU.mult)
+        for cols in pieces:
+            nc.vector.scalar_tensor_tensor(total[:, cols], first[:, cols], SMALL, term1[:, cols], ALU.mult, ALU.add)
+        for cols in pieces:
+            nc.vector.scalar_tensor_tensor(result[:, cols], total[:, cols], 0.0, norm[:, cols], ALU.max, ALU.mult)
+        for cols in pieces:
             nc.sync.dma_start(out=out[:, cols], in_=result[:, cols])

@@ -25,15 +25,17 @@ KIB = 1024
 
 LOW_CUT = 320
 LOW_MID = 416
-MID_CUT = 320
+MID_CUT = 384
 SPLIT = 128
 
 SMALL = 2.0**-32
 CAP = -math.log(SMALL)
 
-AT_PLANE = (5 * KIB, 0, 9 * KIB, 13 * KIB)
-AT_WOVEN = 17 * KIB
-AT_Y = 21 * KIB
+AT_PLANE = (5 * KIB, 0, 13 * KIB, 9 * KIB)
+AT_LOW = 17 * KIB
+AT_W = AT_LOW - KIB // 2
+AT_WOVEN = 20 * KIB
+AT_Y = 24 * KIB
 AT_SCORES = 4 * KIB
 AT_HIGH = KIB // 2
 
@@ -77,7 +79,7 @@ def tile_picked_gatv_relu_e_kernel(tc, xT, w1, score, offs, pos1, pos2, out):
         nc.tensor.transpose(turned[:], score_rows[:], ident[:])
 
         woven = laid.tile([P, PACK * S], BF16, name="woven", offset=AT_WOVEN, align_bytes=64)
-        low_v = keep.tile([P, 2 * LOW_CUT], F32, name="low_v")
+        low_v = laid.tile([P, 2 * LOW_CUT], F32, name="low_v", offset=AT_LOW, align_bytes=64)
         low_s = keep.tile([P, 2 * (S - LOW_CUT)], F32, name="low_s")
         high = laid.tile([P, 2 * S], F32, name="high", offset=AT_HIGH, align_bytes=64)
 
@@ -121,7 +123,7 @@ def tile_picked_gatv_relu_e_kernel(tc, xT, w1, score, offs, pos1, pos2, out):
         nc.gpsimd.tensor_scalar(whole_cols[:], odds_cols[:], SMALL, SMALL, ALU.mult, ALU.add)
 
         for n0, n1 in pieces_v:
-            weave(nc.vector.tensor_copy, 0, low_v, 0, n0, n1)
+            weave(nc.gpsimd.tensor_copy, 0, low_v, 0, n0, n1)
         for n0, n1 in pieces_s:
             weave(nc.scalar.copy, 0, low_s, LOW_CUT, n0, n1)
 
@@ -136,7 +138,7 @@ def tile_picked_gatv_relu_e_kernel(tc, xT, w1, score, offs, pos1, pos2, out):
         weight1 = laid.tile([P, V], F32, name="weight1", offset=AT_PLANE[3], align_bytes=64)
         nc.scalar.activation(weight1[:], odds[:], ACT.Copy, scale=SMALL)
 
-        w_woven = laid.tile([P, PACK * N], BF16, name="w_woven", offset=AT_PLANE[2], align_bytes=64)
+        w_woven = laid.tile([P, PACK * N], BF16, name="w_woven", offset=AT_W, align_bytes=64)
         nc.vector.tensor_copy(
             w_woven[:].rearrange("p (c i j) -> p c j i", i=LINE, j=PACK),
             w_raw[:].rearrange("p j (c i) -> p c j i", i=LINE),

@@ -72,7 +72,7 @@ def tile_picked_gatv_relu_e_kernel(tc, xT, w1, score, offs, pos1, pos2, out):
 
         ident = keep.tile([P, P], F32, name="ident")
         make_identity(nc, ident[:])
-        gap = keep.tile([HALVES, P], F32, name="gap")
+        gap = laid.tile([HALVES, P], F32, name="gap", offset=AT_WOVEN, align_bytes=64)
         nc.gpsimd.tensor_tensor(gap[:], score_raw[:, 1, :], score_raw[:, 0, :], ALU.subtract)
         nc.gpsimd.tensor_scalar_min(score_rows[0:HALVES, :], gap[:], CAP)
         turned = psum.tile([P, P], F32, name="turned")

@@ -26,6 +26,7 @@ KIB = 1024
 LOW_CUT = 320
 LOW_MID = 416
 MID_CUT = 384
+HEAD = 256
 SPLIT = 128
 
 SMALL = 2.0**-32
@@ -55,14 +56,15 @@ def tile_picked_gatv_relu_e_kernel(tc, xT, w1, score, offs, pos1, pos2, out):
         zero = keep.tile([P, 1], F32, name="zero")
         nc.vector.memset(zero[:], 0.0)
         nc.vector.memset(score_rows[0 : P // 2, :], 0.0)
-        nc.scalar.activation(score_rows[P // 2 :, :], zero[P // 2 :, :].to_broadcast([P // 2, P]), ACT.Copy)
 
         x_rows = xT.rearrange("(p j) t -> p j t", j=PACK)
         planes = [laid.tile([P, T], F32, name=f"plane{j}", offset=AT_PLANE[j], align_bytes=64) for j in range(PACK)]
-        nc.sync.dma_start(out=planes[0][:], in_=x_rows[:, 0, :])
+        nc.sync.dma_start(out=planes[0][:, :HEAD], in_=x_rows[:, 0, :HEAD])
+        nc.scalar.dma_start(out=planes[0][:, HEAD:], in_=x_rows[:, 0, HEAD:])
         nc.sync.dma_start(offs_sb[:], offs)
         score_raw = keep.tile([HALVES, D, P], F32, name="score_raw")
         nc.scalar.dma_start(out=score_raw[:], in_=score[:, 0, :].rearrange("d (h c) -> h d c", c=P))
+        nc.scalar.activation(score_rows[P // 2 :, :], zero[P // 2 :, :].to_broadcast([P // 2, P]), ACT.Copy)
         for j in range(1, PACK):
             nc.sync.dma_start(out=planes[j][:], in_=x_rows[:, j, :])
         w_raw = keep.tile([P, PACK, N], F32, name="w_raw")

@@ -26,7 +26,7 @@ KIB = 1024
 LOW_CUT = 320
 LOW_MID = 416
 MID_CUT = 384
-HEAD = 256
+HEAD = 512
 SPLIT = 128
 
 SMALL = 2.0**-32

@@ -27,6 +27,7 @@ LOW_CUT = 320
 LOW_MID = 416
 MID_CUT = 384
 HEAD = 512
+LATE_CUT = 224
 SPLIT = 128
 
 SMALL = 2.0**-32
@@ -131,10 +132,10 @@ def tile_picked_gatv_relu_e_kernel(tc, xT, w1, score, offs, pos1, pos2, out):
 
         gather_v(2, high, 0, 0, MID_CUT)
         gather_s(2, high, 0, MID_CUT, S)
-        gather_v(3, high, 0, 0, 2 * P)
-        for n0 in (3 * P, 2 * P):
-            gather_s(3, high, 0, n0, n0 + P)
-        for n0 in (3 * P, 2 * P):
+        gather_v(3, high, 0, 0, LATE_CUT)
+        for n0, n1 in ((LATE_CUT, 3 * P), (3 * P, S)):
+            gather_s(3, high, 0, n0, n1)
+        for n0 in (2 * P, 3 * P):
             weave(nc.scalar.copy, 2, high, 0, n0, n0 + P)
 
         weight1 = laid.tile([P, V], F32, name="weight1", offset=AT_PLANE[3], align_bytes=64)
@@ -147,7 +148,7 @@ def tile_picked_gatv_relu_e_kernel(tc, xT, w1, score, offs, pos1, pos2, out):
         )
         weave(nc.vector.tensor_copy, 2, high, 0, 0, 2 * P)
 
-        products = ((3 * P, S), (0, P), (P, 2 * P), (2 * P, 3 * P))
+        products = ((2 * P, 3 * P), (0, P), (P, 2 * P), (3 * P, S))
         w_codes = keep.tile([P, N], U32, name="w_codes", align_bytes=64)
         w_scales = keep.tile([P, N], U8, name="w_scales", align_bytes=64)
         nc.vector.quantize_mx(out=w_codes[:].bitcast(FP8X4), scales=w_scales[:], in_=w_woven[:])

import math
from contextlib import ExitStack

import concourse.mybir as mybir
from concourse.masks import make_identity

K, T, S, D, V, N = 512, 1024, 512, 2, 256, 128
FLOPS = 2 * K * N * S

F32 = mybir.dt.float32
BF16 = mybir.dt.bfloat16
U32 = mybir.dt.uint32
U16 = mybir.dt.uint16
U8 = mybir.dt.uint8
FP8X4 = mybir.dt.float8_e4m3fn_x4
ALU = mybir.AluOpType
ACT = mybir.ActivationFunctionType

P = 128
PACK = 4
LINE = 4
GROUP = 16
HALVES = V // P
KIB = 1024

LOW_CUT = 320
LOW_MID = 416
MID_CUT = 384
HEAD = 512
LATE_CUT = 224
SPLIT = 128

SMALL = 2.0**-32
CAP = -math.log(SMALL)

AT_PLANE = (5 * KIB, 0, 13 * KIB, 9 * KIB)
AT_LOW = 17 * KIB
AT_W = AT_LOW - KIB // 2
AT_WOVEN = 20 * KIB
AT_Y = 24 * KIB
AT_SCORES = 4 * KIB
AT_HIGH = KIB // 2


def tile_picked_gatv_relu_e_kernel(tc, xT, w1, score, offs, pos1, pos2, out):
    nc = tc.nc
    with ExitStack() as ctx:
        keep = ctx.enter_context(tc.tile_pool(name="keep", bufs=1))
        laid = ctx.enter_context(tc.tile_pool(name="laid", bufs=1))
        psum = ctx.enter_context(tc.psum_pool(name="psum", bufs=1))

        offs_sb = keep.tile([P, S // GROUP], U16, name="offs_sb")
        pos1_sb = keep.tile([P, V // GROUP], U16, name="pos1_sb")
        pos2_sb = keep.tile([P, V // GROUP], U16, name="pos2_sb")

        score_rows = laid.tile([P, P], F32, name="score_rows", offset=AT_SCORES, align_bytes=64)
        zero = keep.tile([P, 1], F32, name="zero")
        nc.vector.memset(zero[:], 0.0)
        nc.vector.memset(score_rows[0 : P // 2, :], 0.0)

        x_rows = xT.rearrange("(p j) t -> p j t", j=PACK)
        planes = [laid.tile([P, T], F32, name=f"plane{j}", offset=AT_PLANE[j], align_bytes=64) for j in range(PACK)]
        nc.sync.dma_start(out=planes[0][:, :HEAD], in_=x_rows[:, 0, :HEAD])
        nc.scalar.dma_start(out=planes[0][:, HEAD:], in_=x_rows[:, 0, HEAD:])
        nc.sync.dma_start(offs_sb[:], offs)
        score_raw = keep.tile([HALVES, D, P], F32, name="score_raw")
        nc.scalar.dma_start(out=score_raw[:], in_=score[:, 0, :].rearrange("d (h c) -> h d c", c=P))
        nc.scalar.activation(score_rows[P // 2 :, :], zero[P // 2 :, :].to_broadcast([P // 2, P]), ACT.Copy)
        for j in range(1, PACK):
            nc.sync.dma_start(out=planes[j][:], in_=x_rows[:, j, :])
        w_raw = keep.tile([P, PACK, N], F32, name="w_raw")
        nc.sync.dma_start(out=w_raw[:], in_=w1.rearrange("(p j) m -> p j m", j=PACK))
        nc.sync.dma_start(pos2_sb[:], pos2)
        nc.sync.dma_start(pos1_sb[:], pos1)

        ident = keep.tile([P, P], F32, name="ident")
        make_identity(nc, ident[:])
        gap = laid.tile([HALVES, P], F32, name="gap", offset=AT_WOVEN, align_bytes=64)
        nc.gpsimd.tensor_tensor(gap[:], score_raw[:, 1, :], score_raw[:, 0, :], ALU.subtract)
        nc.gpsimd.tensor_scalar_min(score_rows[0:HALVES, :], gap[:], CAP)
        turned = psum.tile([P, P], F32, name="turned")
        nc.tensor.transpose(turned[:], score_rows[:], ident[:])

        woven = laid.tile([P, PACK * S], BF16, name="woven", offset=AT_WOVEN, align_bytes=64)
        low_v = laid.tile([P, 2 * LOW_CUT], F32, name="low_v", offset=AT_LOW, align_bytes=64)
        low_s = keep.tile([P, 2 * (S - LOW_CUT)], F32, name="low_s")
        high = laid.tile([P, 2 * S], F32, name="high", offset=AT_HIGH, align_bytes=64)

        def both_planes(gathered, first, n0, n1):
            return gathered[:].rearrange("p (e n) -> p e n", e=2)[:, :, n0 - first : n1 - first]

        def picked_nodes(j, n0, n1):
            return planes[j][:].indirect(offs_sb[:, n0 // GROUP : n1 // GROUP])

        def gather_v(j, gathered, first, n0, n1):
            nc.vector.tensor_copy(both_planes(gathered, first, n0, n1)[:, j % 2, :], picked_nodes(j, n0, n1))

        def gather_s(j, gathered, first, n0, n1):
            nc.scalar.activation(both_planes(gathered, first, n0, n1)[:, j % 2, :], picked_nodes(j, n0, n1), ACT.Copy)

        def weave(copy, j, gathered, first, n0, n1):
            copy(
                woven[:].rearrange("p (n j) -> p n j", j=PACK)[:, n0:n1, j : j + 2],
                both_planes(gathered, first, n0, n1).rearrange("p e n -> p n e"),
            )

        gather_v(0, low_v, 0, 0, LOW_CUT)
        gather_s(0, low_s, LOW_CUT, LOW_CUT, S)
        pieces_v = ((0, LOW_CUT - P), (LOW_CUT - P, LOW_CUT))
        pieces_s = ((LOW_CUT, LOW_MID), (LOW_MID, S))
        for n0, n1 in pieces_v:
            gather_v(1, low_v, 0, n0, n1)
        for n0, n1 in pieces_s:
            gather_s(1, low_s, LOW_CUT, n0, n1)

        def spread(cols, name):
            rows = psum.tile([P, V], F32, name=name)
            for h in range(HALVES):
                nc.tensor.transpose(rows[:, h * P : (h + 1) * P], cols[:, h : h + 1].to_broadcast([P, P]), ident[:])
            return rows

        odds_cols = laid.tile([P, HALVES], F32, name="odds_cols", offset=AT_PLANE[1], align_bytes=64)
        nc.scalar.activation(odds_cols[:], turned[:, 0:HALVES], ACT.Exp)
        odds = spread(odds_cols, "odds")
        whole_cols = keep.tile([P, HALVES], F32, name="whole_cols")
        nc.gpsimd.tensor_scalar(whole_cols[:], odds_cols[:], SMALL, SMALL, ALU.mult, ALU.add)

        for n0, n1 in pieces_v:
            weave(nc.gpsimd.tensor_copy, 0, low_v, 0, n0, n1)
        for n0, n1 in pieces_s:
            weave(nc.scalar.copy, 0, low_s, LOW_CUT, n0, n1)

        gather_v(2, high, 0, 0, MID_CUT)
        gather_s(2, high, 0, MID_CUT, S)
        gather_v(3, high, 0, 0, LATE_CUT)
        for n0, n1 in ((LATE_CUT, 3 * P), (3 * P, S)):
            gather_s(3, high, 0, n0, n1)
        for n0 in (2 * P, 3 * P):
            weave(nc.scalar.copy, 2, high, 0, n0, n0 + P)

        weight1 = laid.tile([P, V], F32, name="weight1", offset=AT_PLANE[3], align_bytes=64)
        nc.scalar.activation(weight1[:], odds[:], ACT.Copy, scale=SMALL)

        w_woven = laid.tile([P, PACK * N], BF16, name="w_woven", offset=AT_W, align_bytes=64)
        nc.vector.tensor_copy(
            w_woven[:].rearrange("p (c i j) -> p c j i", i=LINE, j=PACK),
            w_raw[:].rearrange("p j (c i) -> p c j i", i=LINE),
        )
        weave(nc.vector.tensor_copy, 2, high, 0, 0, 2 * P)

        products = ((2 * P, 3 * P), (0, P), (P, 2 * P), (3 * P, S))
        w_codes = keep.tile([P, N], U32, name="w_codes", align_bytes=64)
        w_scales = keep.tile([P, N], U8, name="w_scales", align_bytes=64)
        nc.vector.quantize_mx(out=w_codes[:].bitcast(FP8X4), scales=w_scales[:], in_=w_woven[:])
        codes, scales = [], []
        for g, (n0, n1) in enumerate(products):
            codes.append(keep.tile([P, n1 - n0], U32, name=f"codes{g}", align_bytes=64))
            scales.append(keep.tile([P, n1 - n0], U8, name=f"scales{g}", align_bytes=64))
            values = woven[:, PACK * n0 : PACK * n1]
            nc.vector.quantize_mx(out=codes[g][:].bitcast(FP8X4), scales=scales[g][:], in_=values)

        norm_cols = laid.tile([P, HALVES], F32, name="norm_cols", offset=AT_WOVEN, align_bytes=64)
        nc.vector.reciprocal(norm_cols[:], whole_cols[:])

        y = laid.tile([P, S], F32, name="y", offset=AT_Y, align_bytes=64)
        for g, (n0, n1) in enumerate(products):
            acc = psum.tile([P, n1 - n0], F32, name=f"acc{g}")
            nc.tensor.matmul_mx(
                out=acc[:],
                lhsT=w_codes[:].bitcast(FP8X4),
                lhsT_scale=w_scales[:],
                rhs=codes[g][:].bitcast(FP8X4),
                rhs_scale=scales[g][:],
                start=True,
                stop=True,
            )
            nc.scalar.copy(y[:, n0:n1], acc[:])

        norm = spread(norm_cols, "norm")
        pieces = (slice(0, SPLIT), slice(SPLIT, V))
        first = keep.tile([P, V], F32, name="first")
        term1 = keep.tile([P, V], F32, name="term1")
        total = keep.tile([P, V], F32, name="total")
        result = laid.tile([P, V], F32, name="result", offset=AT_Y, align_bytes=64)

        def neighbours(places, cols):
            return y[:].indirect(places[:, cols.start // GROUP : cols.stop // GROUP])

        for cols in pieces:
            nc.scalar.activation(first[:, cols], neighbours(pos1_sb, cols), ACT.Copy)
            nc.vector.tensor_tensor(term1[:, cols], neighbours(pos2_sb, cols), weight1[:, cols], ALU.mult)
        for cols in pieces:
            nc.vector.scalar_tensor_tensor(total[:, cols], first[:, cols], SMALL, term1[:, cols], ALU.mult, ALU.add)
        for cols in pieces:
            nc.vector.scalar_tensor_tensor(result[:, cols], total[:, cols], 0.0, norm[:, cols], ALU.max, ALU.mult)
        for cols in pieces:
            nc.sync.dma_start(out=out[:, cols], in_=result[:, cols])
